import numpy as np, ml_dtypes
CORES = [24,25,26,27,28,29,30,31]
N = 8
BF = ml_dtypes.bfloat16
def f(rng, *shape):
    return (rng.standard_normal(shape, dtype=np.float32) * np.exp2(rng.integers(-2, 3, shape[:-1] + (1,)))).astype(BF)
def wide(rng, *shape):
    v = f(rng, *shape).astype(np.float32); k = shape[:-2] + (1, shape[-1])
    return (v * np.exp2(rng.integers(-6, 7, k)) * (rng.random(k) > 0.0625)).astype(BF)
def gentries(a):
    return np.ascontiguousarray(a.reshape(8, 16, -1).transpose(0, 2, 1)).reshape(8, -1)
def gtable(e):
    e = np.asarray(e); return np.ascontiguousarray(e.reshape(8, -1, 16).transpose(0, 2, 1)).reshape(128, -1).astype(np.int32)
Q, CAPP, M, E, D = 256, 48, 2048, 4096, 4
LV, L = [1, 11, 130, 1000], 2000
EMPTY = 2 ** 24 - 1
def cut(rng, n, m, cap, s):
    u = rng.random((m, cap - 1)) + s * rng.random((m, 1))
    return 1 + np.bincount(np.argsort(u.reshape(-1))[:n - m] // (cap - 1), minlength=m)
def tree(rng, lv, n, keys, repeat=False):
    nk = np.sort(rng.integers(0, EMPTY - 16, (16, M)), axis=0) + np.arange(16)[:, None]
    nk[np.arange(16)[:, None] >= rng.integers(1, 17, (1, M))] = EMPTY
    beg = rng.integers(0, E - 15, M); kid = rng.integers(0, M, E)
    ids = np.concatenate([[0], 1 + rng.permutation(M - 1)]); a = np.cumsum([0] + list(lv))
    lev = [ids[a[l]:a[l + 1]] for l in range(D)]; nxt = lev[1:] + [rng.integers(0, M, n) if repeat else rng.permutation(M)[:n]]
    ek = np.asarray(keys); sizes = []
    for l in range(D - 1, -1, -1):
        sz = cut(rng, len(ek), lv[l], 16, 2.0); st = np.cumsum(sz) - sz
        nk[:, lev[l]] = EMPTY; nk[np.arange(len(ek)) - np.repeat(st, sz), np.repeat(lev[l], sz)] = ek
        ek = ek[st]; sizes.insert(0, sz)
    S = np.concatenate(sizes); C = np.concatenate(nxt); t = len(C); m = len(S)
    o = rng.permutation(m); so = S[o]; st = np.zeros(m, np.int64)
    st[o] = np.cumsum(so) - so + np.sort(rng.integers(0, E - 16 - t + 1, m))
    beg[ids[:m]] = st; kid[np.repeat(st - (np.cumsum(S) - S), S) + np.arange(t)] = C
    return nk, beg, kid
def make(rng, shapes=None, ends=False, full=False, alike=False, repeat=False):
    shapes = shapes or [(LV, L)] * N; I = np.int32
    spl = np.sort(rng.integers(0, EMPTY - 16384 * N + 1, (8, N - 1)), axis=1) + 16384 * np.arange(1, N)
    spl = np.concatenate([np.zeros((8, 1), np.int64), spl], axis=1); hi = np.concatenate([spl[:, 1:], np.full((8, 1), EMPTY)], axis=1)
    nk = np.zeros((N, 128, M), I); beg = np.zeros((N, 8, M), I); kid = np.zeros((N, 8, E), I); sk = np.zeros((N, 8, M), np.int64); ln = np.array([n for _, n in shapes])
    for r in range(N):
        lv, n = shapes[r]
        for g in range(8):
            w = int(hi[g, r] - spl[g, r])
            if ends: k = np.arange(n) + (w - n) * (r % 2)
            else: k = np.sort(rng.integers(0, w - n + 1, n)) + np.arange(n)
            k[0] = 0; k = k + spl[g, r]; sk[r, g, :n] = k
            nk[r, 16 * g:16 * g + 16], beg[r, g], kid[r, g] = tree(rng, lv, n, k, repeat)
    q = np.zeros((N, 8, Q), np.int64)
    for r in range(N):
        for g in range(8):
            if full: cn = np.zeros(N, np.int64); cn[rng.permutation(N)] = np.clip(Q - CAPP * np.arange(N), 0, CAPP)
            else: cn = 3 + cut(rng, Q - 3 * N, N, CAPP - 3, 0.5)
            own = np.repeat(np.arange(N), cn); st = np.cumsum(cn) - cn; occ = np.arange(Q) - st[own]
            a = spl[g, own]; b = hi[g, own]; k = sk[own, g, np.floor(rng.random(Q) * ln[own]).astype(np.int64)]
            inside = a + np.floor(rng.random(Q) * (b - a)).astype(np.int64)
            kd = 1 + occ % 4 if ends else np.array([0, 0, 0, 0, 0, 1, 1, 1, 2, 2, 2, 3, 4])[rng.integers(0, 13, Q)]
            v = np.choose(kd, [inside, k, np.maximum(k - 1, a), a, b - 1])
            if alike: v = v[st[own]]
            q[r, g] = v[rng.permutation(Q)]
    return {"nk": nk, "beg": beg, "kid": kid, "vec": f(rng, N, 128, M), "spl": np.stack([spl.astype(I)] * N), "q": np.stack([gtable(x) for x in q])}
def setup_inputs(rng):
    return make(rng)
def setup_inputs_caps(rng):
    return make(rng, full=True)
def setup_inputs_ends(rng):
    return make(rng, ends=True)
def setup_inputs_shapes(rng):
    a = []; n = M
    for l in range(D): n = -(-n // 16); a.insert(0, n)
    k = M * 3 // 8; b = [min(16 ** l, k) for l in range(D)]; s = int(rng.integers(0, 2))
    return make(rng, shapes=[(a, M) if (r + s) % 2 else (b, k) for r in range(N)], repeat=True)
def setup_inputs_alike(rng):
    return make(rng, alike=True)
def setup_inputs_spread(rng):
    d = make(rng); d["vec"] = wide(rng, N, 128, M); return d
def check_inputs(d):
    bad = []; nk, beg, kid, spl, q = [np.asarray(d[x]).astype(np.int64) for x in ("nk", "beg", "kid", "spl", "q")]
    if not np.isfinite(np.asarray(d["vec"]).astype(np.float32)).all(): bad.append("finite")
    if any(bool((a < 0).any() or (a > b).any()) for a, b in ((nk, EMPTY), (beg, E - 16), (kid, M - 1), (spl, EMPTY - 1), (q, EMPTY - 1))): return bad + ["ranges"]
    if (spl != spl[:1]).any() or (spl[:, :, 0] != 0).any() or (np.diff(spl, axis=2) <= 0).any(): return bad + ["splitters"]
    n4 = nk.reshape(N, 8, 16, M)
    if ((n4[:, :, 1:] <= n4[:, :, :-1]) & (n4[:, :, 1:] < EMPTY)).any(): bad.append("nodes")
    ok = True
    for r in range(N):
        for g in range(8):
            nd = np.zeros(1, np.int64); ek = spl[r, g, r:r + 1]; seen = [nd]
            for l in range(D):
                k = n4[r, g][:, nd].T
                if len(nd) > M or (k[:, 0] != ek).any(): ok = False; break
                use = k < EMPTY; ek = k[use]; nd = kid[r, g][(beg[r, g][nd][:, None] + np.arange(16))[use]]
                if l < D - 1:
                    seen.append(nd)
                    if len(nd) > M: ok = False; break
            if not ok: break
            s = np.concatenate(seen); top = spl[r, g, r + 1] if r + 1 < N else EMPTY
            if len(np.unique(s)) != len(s) or (np.diff(ek) <= 0).any() or ek[-1] >= top: ok = False
        if not ok: break
    if not ok: bad.append("tree")
    for r in range(N):
        x = gentries(q[r]); own = np.sum(x[:, :, None] >= spl[r][:, None, :], axis=2) - 1
        if any(np.bincount(own[g], minlength=N).max() > CAPP for g in range(8)): bad.append("caps"); break
    return bad
def reference(nk, beg, kid, vec, spl, q):
    y = np.zeros((N, 128, Q), vec.dtype); G = np.arange(8)[:, None]
    n4 = nk.reshape(N, 8, 16, M); v4 = vec.reshape(N, 8, 16, M)
    for r in range(N):
        x = gentries(q[r])
        own = np.sum(x[:, :, None] >= spl[r][:, None, :], axis=2) - 1
        at = np.zeros((8, Q), np.int64)
        for l in range(D):
            c = np.sum(n4[own, G, :, at] <= x[:, :, None], axis=2)
            at = kid[own, G, beg[own, G, at] + c - 1]
        y[r] = v4[own, G, :, at].transpose(0, 2, 1).reshape(128, Q)
    return {"y": y}

@@ -1,0 +1,274 @@
+from concourse.bass import DstId, RemoteDMATransfer
+from concourse.mybir import dt, AluOpType, ActivationFunctionType
+
+N, Q, CAP, M, E, D = 8, 256, 48, 2048, 4096, 4
+S = N * CAP
+H = S // 2
+OWN = S - CAP
+KW = E - 15
+BIG = 2 ** 24
+VC = 48
+NA = 1344
+
+SCRATCH = {
+    "qrep": ("sbuf", [128, Q], "int32"),
+    "spc": ("sbuf", [128, 1], "int32"),
+    "lof": ("sbuf", [128, 1], "float32"),
+    "kp": ("sbuf", [128, 1], "int32"),
+    "kq": ("sbuf", [128, 1], "int32"),
+    "basec": ("sbuf", [128, 1], "float32"),
+    "ones": ("sbuf", [128, Q], "bfloat16"),
+    "idn": ("sbuf", [128, 128], "bfloat16"),
+    "sup": ("sbuf", [128, 128], "bfloat16"),
+    "sub": ("sbuf", [128, 128], "bfloat16"),
+    "eg0": ("sbuf", [128, 8], "bfloat16"),
+    "eg": ("sbuf", [128, 8], "bfloat16"),
+    "bz": ("sbuf", [128, 144], "bfloat16"),
+    "bsel": ("sbuf", [128, 144], "float16"),
+    "dm": ("sbuf", [128, 128], "float16"),
+    "em": ("sbuf", [128, 128], "float16"),
+    "ge": ("sbuf", [128, Q], "float16"),
+    "pos": ("sbuf", [128, Q], "float16"),
+    "w": ("sbuf", [128, Q], "float16"),
+    "off1": ("sbuf", [128, 16], "uint16"),
+    "off2": ("sbuf", [128, 16], "uint16"),
+    "z": ("sbuf", [128, S + OWN], "int32"),
+    "kids": ("sbuf", [128, KW], "int32"),
+    "bt": ("sbuf", [128, 128], "int32"),
+    "bx": ("sbuf", [128, 128], "float32"),
+    "by": ("sbuf", [128, 128], "float32"),
+    "boff": ("sbuf", [128, 128], "uint16"),
+    "cz": ("sbuf", [128, 32], "float16"),
+    "ct": ("sbuf", [128, M], "float32"),
+    "d0": ("sbuf", [128, 1], "float32"),
+    "nk0": ("sbuf", [128, 8], "int32"),
+    "key0": ("sbuf", [128, 1], "float32"),
+    "nkw": ("sbuf", [128, M], "int32"),
+    "vw": ("sbuf", [128, M], "bfloat16"),
+    "cmp": ("sbuf", [128, D * S], "float16"),
+    "cg": ("sbuf", [128, D * S], "float16"),
+    "pr": ("sbuf", [128, D * S], "float16"),
+    "offs": ("sbuf", [128, D * 32], "uint16"),
+    "yb": ("sbuf", [128, S + OWN], "bfloat16"),
+    "ysb": ("sbuf", [128, Q], "bfloat16"),
+    "psM": ("psum", [128, 512], "float32"),
+    "psL": ("psum", [128, 512], "float32"),
+    "psA": ("psum", [128, 512], "float32"),
+    "psB": ("psum", [128, 512], "float32"),
+    "psP": ("psum", [128, 512], "float32"),
+    "psQ": ("psum", [128, 512], "float32"),
+}
+SEMAPHORES = ["e%d" % i for i in range(120)] + ["qin", "splin", "kidin", "btin", "nkin", "arrA", "arrB", "retA", "retB", "sent"]
+
+
+def rank_program(g, core, T, topo):
+    me = T.rank_of(core)
+    if me is None:
+        return
+    A = AluOpType
+    V, P, S_, SY = g.vector, g.tensor, g.scalar, g.sync
+    COPY = ActivationFunctionType.Copy
+    cnt = [0]
+
+    def ev():
+        cnt[0] += 1
+        return T.sem["e%d" % (cnt[0] - 1)]
+
+    def do(instr, n=1):
+        e = ev()
+        instr.then_inc(e, n)
+        return (e, n)
+
+    def wait(q, *events):
+        for e, n in events:
+            q.wait_ge(e, n)
+
+    def kid_load(q, o):
+        q.dma_start(T.kids[o::16, :], T.kid[:, o:o + KW]).then_inc(T.sem.kidin, 16)
+
+    e_spc = do(V.memset(T.spc[:], BIG))
+    kid_load(SY, 0)
+    for h in range(2):
+        S_.dma_start(T.bt[:, 64 * h:64 * h + 64], T.beg[h::2, :]).then_inc(T.sem.btin, 16)
+    for o in range(8):
+        SY.dma_start(T.qrep[o::16, :], T.q[:]).then_inc(T.sem.qin, 16)
+        S_.dma_start(T.qrep[o + 8::16, :], T.q[:]).then_inc(T.sem.qin, 16)
+    wait(SY, e_spc)
+    wait(S_, e_spc)
+    for x in range(8):
+        (SY if x < 4 else S_).dma_start(T.spc[16 * x:16 * x + 8, 0:1], T.spl[x, :]).then_inc(T.sem.splin, 16)
+    e_nk0 = do(SY.dma_start(T.nk0[:], T.nk[:, 0:8]), 16)
+    for o in range(1, 16):
+        kid_load(S_ if o % 2 and o < 15 else SY, o)
+    SY.dma_start(T.nkw[:, 0:NA], T.nk[:, 0:NA]).then_inc(T.sem.nkin, 16)
+    q_in, spl_in, kid_in, bt_in, nk_in = (T.sem.qin, 256), (T.sem.splin, 128), (T.sem.kidin, 256), (T.sem.btin, 32), (T.sem.nkin, 32)
+
+    e_ones = do(V.memset(T.ones[:], 1.0))
+    e_bz = do(V.memset(T.bz[:], 0.0))
+    e_z0 = do(V.memset(T.z[:, 0:S], 0))
+    wait(g, e_ones)
+    e_idn = do(g.affine_select(T.idn[:], T.ones[:, 0:128], [[-1, 128]], A.is_equal, 0.0, 0, 1))
+    e_sub = do(g.affine_select(T.sub[:], T.ones[:, 0:128], [[-1, 128]], A.is_equal, 0.0, -1, 1))
+    e_kp = do(g.iota(T.kp[:], [[0, 1]], 128 - me - 1, 1))
+    e_eg0 = do(g.affine_select(T.eg0[:], T.ones[:, 0:8], [[-16, 8]], A.is_ge, 0.0, 0, 1))
+    wait(g, e_eg0)
+    e_eg = do(g.affine_select(T.eg[:], T.eg0[:], [[16, 8]], A.is_ge, 0.0, 15, -1))
+    e_sup = do(g.affine_select(T.sup[:], T.ones[:, 0:128], [[-1, 128]], A.is_equal, 0.0, 1, 1))
+    wait(V, e_sub)
+    e = do(V.memset(T.sub[:, 15::16], 0.0))
+    wait(V, e, e_idn)
+    e_em = do(V.tensor_tensor(out=T.em[:], in0=T.idn[:], in1=T.sub[:], op=A.subtract))
+    wait(V, e_kp)
+    e = do(V.tensor_scalar(out=T.kq[:], in0=T.kp[:], scalar1=7, scalar2=None, op0=A.bitwise_and))
+    wait(V, e)
+    e_base = do(V.tensor_scalar(out=T.basec[:], in0=T.kq[:], scalar1=float(CAP), scalar2=-1.0, op0=A.mult, op1=A.add))
+
+    def to_list(ps, cols):
+        for i in range(16):
+            m = P.matmul(ps, T.bsel[:, 15 - i:143 - i], cols(i), i == 0, i == 15)
+        return do(m)
+
+    wait(S_, bt_in)
+    e_bx = []
+    for h in range(2):
+        for b in range(4):
+            e_bx.append(do(S_.activation(T.bx[:, 32 * b + 16 * h:32 * b + 16 * h + 16], T.bt[:, 64 * h + 16 * b:64 * h + 16 * b + 16], COPY)))
+
+    wait(V, spl_in)
+    e = do(V.tensor_copy(out=T.lof[:], in_=T.spc[:]))
+    wait(V, e, q_in)
+    e_ge = do(V.tensor_scalar(out=T.ge[:], in0=T.qrep[:], scalar1=T.lof[:], scalar2=None, op0=A.is_ge))
+    wait(P, e_em, e_ge)
+    e_mask = do(P.matmul(T.psM[:, 0:Q], T.em[:], T.ge[:], True, True))
+    wait(V, e_eg, e_bz)
+    e = do(V.tensor_copy(out=T.bz[:, 15:143:16], in_=T.eg[:]))
+    wait(V, e)
+    e_bsel = do(V.tensor_copy(out=T.bsel[:], in_=T.bz[:]))
+    wait(V, e_mask, e_base)
+    e = do(V.tensor_tensor_scan(T.pos[:], T.ones[:], T.psM[:, 0:Q], T.basec[:], A.mult, A.add))
+    wait(V, e)
+    e_w = do(V.tensor_tensor(out=T.w[:], in0=T.psM[:, 0:Q], in1=T.pos[:], op=A.mult))
+    wait(P, e_w, e_bsel)
+    e_l1 = to_list(T.psL[:, 0:16], lambda i: T.w[:, i::16])
+    wait(V, *e_bx)
+    e_by = do(V.transpose(T.by[:], T.bx[:]))
+    wait(V, e_l1)
+    e_off1 = do(V.tensor_copy(out=T.off1[:], in_=T.psL[:, 0:16]))
+    wait(V, e_off1, e_z0)
+    e_sc = do(V.tensor_copy(out=T.z[:, 0:S].indirect(T.off1[:, 0:16]), in_=T.qrep[:]))
+    wait(P, e_off1)
+    e_l2 = to_list(T.psL[:, 16:32], lambda i: T.w[:, 16 * i:16 * i + 16])
+    wait(S_, e_by)
+    e_bo = [do(S_.activation(T.boff[:, b::4], T.by[:, 32 * b:32 * b + 32], COPY)) for b in range(4)]
+
+    def transfer(buf, src_col, dst_col, peer, n, slot, sem):
+        dst = T.cores[peer]
+        rid, pid, _ = topo.addr(dst)
+        en = topo.engines(core, dst)[n * slot:n * slot + n]
+        return RemoteDMATransfer(dst_ids=[DstId(rid=rid, pnc=pid)], dma_engine_mask=sum(1 << x for x in en), remote_sem=sem,
+                                 src=buf[:, src_col:src_col + CAP], dst=buf[:, dst_col:dst_col + CAP])
+
+    wait(g, e_sc)
+    for ks, sem in (((6, 5, 4), T.sem.arrA), ((3, 2, 1, 0), T.sem.arrB)):
+        g.remote_dma_fused([transfer(T.z, CAP * k, S + CAP * (6 - k), (me + 1 + k) % N, 4, j, sem) for j, k in enumerate(ks)],
+                           local_sem=T.sem.sent)
+    e_go = ev()
+    g.sem_inc(e_go, 1)
+    wait(SY, (e_go, 1))
+    SY.dma_start(T.nkw[:, NA:M], T.nk[:, NA:M]).then_inc(T.sem.nkin, 16)
+    e_vec = do(SY.dma_start(T.vw[:], T.vec[:]), 16)
+
+    wait(V, e_sup)
+    e = do(V.memset(T.sup[:, 0::16], 0.0))
+    wait(V, e)
+    e_dm = do(V.tensor_tensor(out=T.dm[:], in0=T.idn[:], in1=T.sup[:], op=A.subtract))
+    wait(V, e_nk0)
+    e_k0 = do(V.tensor_copy(out=T.key0[:], in_=T.nk0[:, 0:1]))
+    wait(V, e_l2)
+    e_off2 = do(V.tensor_copy(out=T.off2[:], in_=T.psL[:, 16:32]))
+    wait(V, kid_in, *e_bo)
+    e_cz = do(V.tensor_copy(out=T.cz[:], in_=T.kids[:].indirect(T.boff[:, 0:2])))
+    e_ct = do(V.tensor_copy(out=T.ct[:, 0:16 * VC], in_=T.kids[:].indirect(T.boff[:, 0:VC])))
+    wait(S_, kid_in, *e_bo)
+    e_cs = do(S_.activation(T.ct[:, 16 * VC:M], T.kids[:].indirect(T.boff[:, VC:128]), COPY))
+    wait(P, e_cz, e_dm)
+    e_p0 = do(P.matmul(T.psM[:, 256:257], T.dm[:], T.cz[:, 0:1], True, True))
+    wait(V, e_p0)
+    e_d0 = do(V.tensor_copy(out=T.d0[:], in_=T.psM[:, 256:257]))
+
+    X = (T.z[:, OWN:OWN + H], T.z[:, OWN + H:OWN + S])
+    ps = (T.psA, T.psB)
+    po = (T.psP, T.psQ)
+    arr = ((T.sem.arrA, 12), (T.sem.arrB, 16))
+
+    def col(buf, l, h):
+        return buf[:, S * l + H * h:S * l + H * h + H]
+
+    def spread(l, h, e_pr):
+        wait(P, e_pr)
+        b = S * l + H * h
+        return to_list(ps[h][:, 16 * l:16 * l + 12], lambda i: T.pr[:, b + i:b + H:16])
+
+    def offsets(l, h):
+        o = T.offs[:, 32 * (l - 1) + 16 * h:32 * (l - 1) + 16 * h + 12]
+        wait(V, lst[h])
+        return o, do(V.tensor_copy(out=o, in_=ps[h][:, 16 * (l - 1):16 * (l - 1) + 12]))
+
+    def compare(l, h, o, e_o):
+        wait(S_, e_o)
+        if l == 1 and h == 0:
+            wait(S_, e_ct, e_cs)
+        e_g = do(S_.activation(col(T.cg, l, h), T.ct[:].indirect(o), COPY))
+        wait(V, e_o)
+        if l == 1 and h == 0:
+            wait(V, nk_in)
+        e_c = do(V.tensor_tensor(out=col(T.cmp, l, h), in0=T.nkw[:].indirect(o), in1=X[h], op=A.is_le))
+        wait(P, e_c)
+        return e_g, do(P.matmul(po[h][:, 0:H], T.em[:], col(T.cmp, l, h), True, True))
+
+    def pick(l, h, e_g, e_one):
+        wait(V, e_g, e_one)
+        return do(V.tensor_tensor(out=col(T.pr, l, h), in0=po[h][:, 0:H], in1=col(T.cg, l, h), op=A.mult))
+
+    lst = [None, None]
+    wait(V, e_k0, e_d0)
+    for h in range(2):
+        wait(V, arr[h])
+        e_pr = do(V.tensor_scalar(out=col(T.pr, 0, h), in0=X[h], scalar1=T.key0[:], scalar2=T.d0[:], op0=A.is_ge, op1=A.mult))
+        lst[h] = spread(0, h, e_pr)
+    for l in range(1, D):
+        es = [compare(l, h, *offsets(l, h)) for h in range(2)]
+        for h in range(2):
+            lst[h] = spread(l, h, pick(l, h, *es[h]))
+    offs = []
+    for h in range(2):
+        o, e_o = offsets(D, h)
+        out = OWN + H * h
+        if h == 0:
+            wait(S_, e_o, e_vec)
+            e_y = [do(S_.activation(T.yb[:, out:out + H], T.vw[:].indirect(o), COPY))]
+        else:
+            b = 32 * (D - 1) + 16 * h
+            wait(S_, e_o, e_vec)
+            e_y = [do(S_.activation(T.yb[:, out + H // 2:out + H], T.vw[:].indirect(T.offs[:, b + 6:b + 12]), COPY))]
+            wait(V, e_o, e_vec)
+            e_y.append(do(V.tensor_copy(out=T.yb[:, out:out + H // 2], in_=T.vw[:].indirect(T.offs[:, b:b + 6]))))
+        wait(g, *e_y)
+        sem = (T.sem.retA, T.sem.retB)[h]
+        g.remote_dma_fused([transfer(T.yb, S + CAP * k, CAP * (6 - k), (me + 1 + k) % N, 4, j, sem)
+                            for j, k in enumerate(((0, 1, 2), (3, 4, 5, 6))[h])], local_sem=T.sem.sent)
+        offs += e_y
+
+    for j, (q, dq) in enumerate(((V, SY), (S_, S_))):
+        wait(q, *offs)
+        wait(q, (T.sem.retA, 12), (T.sem.retB, 16), e_off2)
+        c = slice(128 * j, 128 * j + 128)
+        src = T.yb[:, 0:S].indirect(T.off2[:, 8 * j:8 * j + 8])
+        if j == 0:
+            e = do(V.tensor_copy(out=T.ysb[:, c], in_=src))
+        else:
+            e = do(S_.activation(T.ysb[:, c], src, COPY))
+        wait(dq, e)
+        e = do(dq.dma_start(T.y[:, c], T.ysb[:, c]), 16)
+        wait(dq, e)
+    g.wait_ge(T.sem.sent, 56)

@@ -4,52 +4,58 @@ from concourse.mybir import dt, AluOpType, ActivationFunctionType
 N, Q, CAP, M, E, D = 8, 256, 48, 2048, 4096, 4
 S = N * CAP
 H = S // 2
-OWN = S - CAP
 KW = E - 15
-BIG = 2 ** 24
 VC = 48
 NA = 1344
 
 SCRATCH = {
+    "qi": ("sbuf", [128, Q], "int32"),
+    "qf": ("sbuf", [128, Q], "float32"),
     "qrep": ("sbuf", [128, Q], "int32"),
     "spc": ("sbuf", [128, 1], "int32"),
     "lof": ("sbuf", [128, 1], "float32"),
     "kp": ("sbuf", [128, 1], "int32"),
-    "kq": ("sbuf", [128, 1], "int32"),
-    "basec": ("sbuf", [128, 1], "float32"),
-    "ones": ("sbuf", [128, Q], "bfloat16"),
-    "idn": ("sbuf", [128, 128], "bfloat16"),
-    "sup": ("sbuf", [128, 128], "bfloat16"),
-    "sub": ("sbuf", [128, 128], "bfloat16"),
-    "eg0": ("sbuf", [128, 8], "bfloat16"),
-    "eg": ("sbuf", [128, 8], "bfloat16"),
-    "bz": ("sbuf", [128, 144], "bfloat16"),
+    "kq": ("sbuf", [128, 8], "int32"),
+    "cols": ("sbuf", [128, 16], "float32"),
+    "sel": ("sbuf", [128, 192], "float32"),
+    "rep": ("sbuf", [128, 128], "float32"),
+    "jd": ("sbuf", [128, 160], "bfloat16"),
+    "ones": ("sbuf", [128, 192], "bfloat16"),
+    "m3": ("sbuf", [128, 3 * 128], "float16"),
+    "b8": ("sbuf", [128, 160], "float16"),
     "bsel": ("sbuf", [128, 144], "float16"),
-    "dm": ("sbuf", [128, 128], "float16"),
+    "neg": ("sbuf", [128, 128], "bfloat16"),
+    "emb": ("sbuf", [128, 128], "bfloat16"),
     "em": ("sbuf", [128, 128], "float16"),
-    "ge": ("sbuf", [128, Q], "float16"),
-    "pos": ("sbuf", [128, Q], "float16"),
-    "w": ("sbuf", [128, Q], "float16"),
+    "idn": ("sbuf", [128, 128], "float16"),
+    "ge": ("sbuf", [128, 128], "float16"),
+    "cum": ("sbuf", [128, 128], "float16"),
+    "w": ("sbuf", [128, 128], "float16"),
     "off1": ("sbuf", [128, 16], "uint16"),
     "off2": ("sbuf", [128, 16], "uint16"),
-    "z": ("sbuf", [128, S + OWN], "int32"),
+    "z": ("sbuf", [128, S], "int32"),
+    "xs": ("sbuf", [128, S], "int32"),
     "kids": ("sbuf", [128, KW], "int32"),
     "bt": ("sbuf", [128, 128], "int32"),
     "bx": ("sbuf", [128, 128], "float32"),
     "by": ("sbuf", [128, 128], "float32"),
     "boff": ("sbuf", [128, 128], "uint16"),
-    "cz": ("sbuf", [128, 32], "float16"),
+    "l2": ("sbuf", [128, 32], "uint16"),
+    "l3": ("sbuf", [128, 32], "uint16"),
+    "k2": ("sbuf", [128, 32], "int32"),
+    "k3": ("sbuf", [128, 256], "int32"),
+    "c3": ("sbuf", [128, 256], "float32"),
     "ct": ("sbuf", [128, M], "float32"),
-    "d0": ("sbuf", [128, 1], "float32"),
-    "nk0": ("sbuf", [128, 8], "int32"),
     "key0": ("sbuf", [128, 1], "float32"),
     "nkw": ("sbuf", [128, M], "int32"),
     "vw": ("sbuf", [128, M], "bfloat16"),
     "cmp": ("sbuf", [128, D * S], "float16"),
     "cg": ("sbuf", [128, D * S], "float16"),
     "pr": ("sbuf", [128, D * S], "float16"),
+    "up": ("sbuf", [128, 32], "float16"),
     "offs": ("sbuf", [128, D * 32], "uint16"),
-    "yb": ("sbuf", [128, S + OWN], "bfloat16"),
+    "yo": ("sbuf", [128, S], "bfloat16"),
+    "ret": ("sbuf", [128, S], "bfloat16"),
     "ysb": ("sbuf", [128, Q], "bfloat16"),
     "psM": ("psum", [128, 512], "float32"),
     "psL": ("psum", [128, 512], "float32"),
@@ -58,7 +64,7 @@ SCRATCH = {
     "psP": ("psum", [128, 512], "float32"),
     "psQ": ("psum", [128, 512], "float32"),
 }
-SEMAPHORES = ["e%d" % i for i in range(120)] + ["qin", "splin", "kidin", "btin", "nkin", "arrA", "arrB", "retA", "retB", "sent"]
+SEMAPHORES = ["e%d" % i for i in range(136)] + ["splin", "kidin", "btin", "arrA", "arrB", "retA", "retB", "sent"]
 
 
 def rank_program(g, core, T, topo):
@@ -67,136 +73,153 @@ def rank_program(g, core, T, topo):
         return
     A = AluOpType
     V, P, S_, SY = g.vector, g.tensor, g.scalar, g.sync
-    COPY = ActivationFunctionType.Copy
+    COPY, IDENT = ActivationFunctionType.Copy, ActivationFunctionType.Identity
     cnt = [0]
 
     def ev():
         cnt[0] += 1
         return T.sem["e%d" % (cnt[0] - 1)]
 
-    def do(instr, n=1):
+    def do(*instrs, n=1):
         e = ev()
-        instr.then_inc(e, n)
-        return (e, n)
+        for i in instrs:
+            i.then_inc(e, n)
+        return (e, n * len(instrs))
 
     def wait(q, *events):
         for e, n in events:
             q.wait_ge(e, n)
 
-    def kid_load(q, o):
-        q.dma_start(T.kids[o::16, :], T.kid[:, o:o + KW]).then_inc(T.sem.kidin, 16)
+    def ts(out, in0, s1, op0, s2=None, op1=None):
+        if op1 is None:
+            return V.tensor_scalar(out=out, in0=in0, scalar1=s1, scalar2=None, op0=op0)
+        return V.tensor_scalar(out=out, in0=in0, scalar1=s1, scalar2=s2, op0=op0, op1=op1)
 
-    e_spc = do(V.memset(T.spc[:], BIG))
-    kid_load(SY, 0)
+    q_in = do(SY.dma_start(T.qi[0:8, :], T.q[:]), n=16)
+    for h in range(2):
+        S_.dma_start(T.spc[64 * h:64 * h + 64, 0:1], T.spl[:]).then_inc(T.sem.splin, 16)
     for h in range(2):
         S_.dma_start(T.bt[:, 64 * h:64 * h + 64], T.beg[h::2, :]).then_inc(T.sem.btin, 16)
-    for o in range(8):
-        SY.dma_start(T.qrep[o::16, :], T.q[:]).then_inc(T.sem.qin, 16)
-        S_.dma_start(T.qrep[o + 8::16, :], T.q[:]).then_inc(T.sem.qin, 16)
-    wait(SY, e_spc)
-    wait(S_, e_spc)
-    for x in range(8):
-        (SY if x < 4 else S_).dma_start(T.spc[16 * x:16 * x + 8, 0:1], T.spl[x, :]).then_inc(T.sem.splin, 16)
-    e_nk0 = do(SY.dma_start(T.nk0[:], T.nk[:, 0:8]), 16)
-    for o in range(1, 16):
-        kid_load(S_ if o % 2 and o < 15 else SY, o)
-    SY.dma_start(T.nkw[:, 0:NA], T.nk[:, 0:NA]).then_inc(T.sem.nkin, 16)
-    q_in, spl_in, kid_in, bt_in, nk_in = (T.sem.qin, 256), (T.sem.splin, 128), (T.sem.kidin, 256), (T.sem.btin, 32), (T.sem.nkin, 32)
+    for o in range(16):
+        SY.dma_start(T.kids[o::16, :], T.kid[:, o:o + KW]).then_inc(T.sem.kidin, 16)
+    nk_a = do(SY.dma_start(T.nkw[:, 0:NA], T.nk[:, 0:NA]), n=16)
+    spl_in, kid_in, bt_in = (T.sem.splin, 32), (T.sem.kidin, 256), (T.sem.btin, 32)
 
-    e_ones = do(V.memset(T.ones[:], 1.0))
-    e_bz = do(V.memset(T.bz[:], 0.0))
-    e_z0 = do(V.memset(T.z[:, 0:S], 0))
-    wait(g, e_ones)
-    e_idn = do(g.affine_select(T.idn[:], T.ones[:, 0:128], [[-1, 128]], A.is_equal, 0.0, 0, 1))
-    e_sub = do(g.affine_select(T.sub[:], T.ones[:, 0:128], [[-1, 128]], A.is_equal, 0.0, -1, 1))
-    e_kp = do(g.iota(T.kp[:], [[0, 1]], 128 - me - 1, 1))
-    e_eg0 = do(g.affine_select(T.eg0[:], T.ones[:, 0:8], [[-16, 8]], A.is_ge, 0.0, 0, 1))
-    wait(g, e_eg0)
-    e_eg = do(g.affine_select(T.eg[:], T.eg0[:], [[16, 8]], A.is_ge, 0.0, 15, -1))
-    e_sup = do(g.affine_select(T.sup[:], T.ones[:, 0:128], [[-1, 128]], A.is_equal, 0.0, 1, 1))
-    wait(V, e_sub)
-    e = do(V.memset(T.sub[:, 15::16], 0.0))
-    wait(V, e, e_idn)
-    e_em = do(V.tensor_tensor(out=T.em[:], in0=T.idn[:], in1=T.sub[:], op=A.subtract))
+    half = (slice(0, 64), slice(64, 128))
+    CA, CB, CC, CU, CI, CT, CS, C16, CR = (T.cols[:, j:j + 1] for j in range(9))
+    e_one = do(V.memset(T.ones[:], 1.0))
+    e_kp = do(g.iota(T.kp[:], [[0, 1]], 0, 1))
+    wait(g, e_one)
+    e_sel = do(g.affine_select(T.sel[0:8, :], T.ones[0:8, :], [[-1, 24], [0, 8]], A.is_equal, 0.0, 8, 1))
+    e_jd = do(g.iota(T.jd[:], [[1, 160]], 0, -1, allow_small_or_imprecise_dtypes=True))
+    e_z0 = do(g.iota(T.z[:], [[0, S]], 0, 0))
+    e_c0 = do(V.memset(T.cols[half[0], 6:7], 1.0), V.memset(T.cols[half[1], 6:7], -1.0))
+    e_neg = do(V.memset(T.neg[:], -1.0))
     wait(V, e_kp)
-    e = do(V.tensor_scalar(out=T.kq[:], in0=T.kp[:], scalar1=7, scalar2=None, op0=A.bitwise_and))
-    wait(V, e)
-    e_base = do(V.tensor_scalar(out=T.basec[:], in0=T.kq[:], scalar1=float(CAP), scalar2=-1.0, op0=A.mult, op1=A.add))
+    e_kq = do(ts(T.kq[:, 0:1], T.kp[:], 7, A.bitwise_and), ts(T.kq[:, 4:5], T.kp[:], 15, A.bitwise_and))
+    wait(V, e_kq, e_neg)
+    R = T.kq[:, 0:1]
+    e_c1 = do(ts(CA, R, 0.0, A.is_gt, 1.0, A.add), ts(CB, R, 0.0, A.is_gt, -1.0, A.mult), ts(CC, R, 7.0, A.is_lt, -1.0, A.mult))
+    e_neg = do(V.memset(T.neg[:, 15::16], 0.0))
+    wait(S_, e_kq)
+    e_u = do(*[S_.activation(T.cols[half[h], 3:4], T.kq[half[h], 0:1], COPY, bias=(25.0, 24.0)[h], scale=(-24.0, 24.0)[h]) for h in range(2)],
+             *[S_.activation(T.cols[half[h], 8:9], T.kq[half[h], 0:1], COPY, bias=16.0 - 127.0 * h, scale=-2.0) for h in range(2)])
 
-    def to_list(ps, cols):
-        for i in range(16):
-            m = P.matmul(ps, T.bsel[:, 15 - i:143 - i], cols(i), i == 0, i == 15)
-        return do(m)
-
-    wait(S_, bt_in)
-    e_bx = []
-    for h in range(2):
-        for b in range(4):
-            e_bx.append(do(S_.activation(T.bx[:, 32 * b + 16 * h:32 * b + 16 * h + 16], T.bt[:, 64 * h + 16 * b:64 * h + 16 * b + 16], COPY)))
-
+    wait(V, q_in)
+    wait(S_, q_in)
+    e_qf = do(V.tensor_copy(out=T.qf[0:8, 0:128], in_=T.qi[0:8, 0:128]), S_.activation(T.qf[0:8, 128:Q], T.qi[0:8, 128:Q], COPY))
+    wait(S_, e_sel, e_u)
+    e_rep = do(*[S_.activation(T.rep[0:8, j::2], T.sel[0:8, 64:128], COPY) for j in range(2)])
+    e_ci = do(S_.activation(CT, T.kp[:], IDENT, bias=CR),
+              *[S_.activation(T.cols[half[h], 4:5], T.kq[half[h], 0:1], COPY, bias=(1336.0, -1728.0)[h], scale=T.cols[half[h], 3:4]) for h in range(2)],
+              S_.activation(C16, T.kq[:, 4:5], COPY, bias=15.0, scale=-1.0))
+    wait(P, e_qf, e_sel)
+    P.matmul(T.psP[:, 0:128], T.sel[0:8, 64:192], T.qf[0:8, 0::2], True, False)
+    e_qh = do(P.matmul(T.psP[:, 0:128], T.sel[0:8, 0:128], T.qf[0:8, 1::2], False, True))
+    wait(P, e_rep)
+    P.matmul(T.psQ[:, 0:128], T.rep[0:8, :], T.qf[0:8, 0:128], True, True)
     wait(V, spl_in)
-    e = do(V.tensor_copy(out=T.lof[:], in_=T.spc[:]))
-    wait(V, e, q_in)
-    e_ge = do(V.tensor_scalar(out=T.ge[:], in0=T.qrep[:], scalar1=T.lof[:], scalar2=None, op0=A.is_ge))
-    wait(P, e_em, e_ge)
-    e_mask = do(P.matmul(T.psM[:, 0:Q], T.em[:], T.ge[:], True, True))
-    wait(V, e_eg, e_bz)
-    e = do(V.tensor_copy(out=T.bz[:, 15:143:16], in_=T.eg[:]))
-    wait(V, e)
-    e_bsel = do(V.tensor_copy(out=T.bsel[:], in_=T.bz[:]))
-    wait(V, e_mask, e_base)
-    e = do(V.tensor_tensor_scan(T.pos[:], T.ones[:], T.psM[:, 0:Q], T.basec[:], A.mult, A.add))
-    wait(V, e)
-    e_w = do(V.tensor_tensor(out=T.w[:], in0=T.psM[:, 0:Q], in1=T.pos[:], op=A.mult))
-    wait(P, e_w, e_bsel)
-    e_l1 = to_list(T.psL[:, 0:16], lambda i: T.w[:, i::16])
-    wait(V, *e_bx)
+    e_lo = do(V.tensor_copy(out=T.lof[:], in_=T.spc[:]))
+    wait(V, e_jd, e_c1)
+    e_m3 = do(*[ts(T.m3[:, 128 * j:128 * j + 128], T.jd[:, 0:128], float(d), A.is_equal, c, A.mult)
+                for j, (d, c) in enumerate(((0, CA), (-1, CB), (1, CC)))])
+    wait(V, e_lo, e_qh)
+    e_ge = do(ts(T.ge[:], T.psP[:, 0:128], T.lof[:], A.is_ge))
+    wait(P, e_m3, e_ge)
+    for j in range(3):
+        m = P.matmul(T.psM[:, 0:128], T.m3[:, 128 * j:128 * j + 128], T.ge[:], j == 0, j == 2)
+    e_mask = do(m)
+    e_qr = do(P.matmul(T.psQ[:, 128:Q], T.rep[0:8, :], T.qf[0:8, 128:Q], True, True))
+    wait(V, e_ge, e_one, e_ci, e_c0)
+    e = do(V.tensor_tensor_scan(T.cum[:], T.ones[:, 0:128], T.ge[:], CI, A.mult, A.add))
+    e_b8 = do(ts(T.b8[:], T.jd[:], CT, A.is_equal, CS, A.mult))
+    wait(V, e, e_mask)
+    e_w = do(V.tensor_tensor(out=T.w[:], in0=T.psM[:, 0:128], in1=T.cum[:], op=A.mult))
+    wait(P, e_w, e_b8)
+    for i in range(8):
+        m = P.matmul(T.psL[:, 0:16], T.b8[:, 16 - 2 * i:144 - 2 * i], T.w[:, i::8], i == 0, i == 7)
+    e_l1 = do(m)
+    wait(S_, bt_in)
+    e_bx = do(*[S_.activation(T.bx[:, 32 * b + 16 * h:32 * b + 16 * h + 16], T.bt[:, 64 * h + 16 * b:64 * h + 16 * b + 16], COPY)
+                for h in range(2) for b in range(4)])
+    wait(V, e_bx)
     e_by = do(V.transpose(T.by[:], T.bx[:]))
+    wait(S_, e_qr)
+    e_ev = do(S_.activation(T.qrep[:], T.psQ[:, 0:Q], COPY))
+    wait(S_, e_by)
+    e_bo = do(*[S_.activation(T.boff[:, b::4], T.by[:, 32 * b:32 * b + 32], COPY) for b in range(4)])
     wait(V, e_l1)
     e_off1 = do(V.tensor_copy(out=T.off1[:], in_=T.psL[:, 0:16]))
-    wait(V, e_off1, e_z0)
-    e_sc = do(V.tensor_copy(out=T.z[:, 0:S].indirect(T.off1[:, 0:16]), in_=T.qrep[:]))
+    wait(V, e_off1, e_z0, e_ev)
+    e_sc = do(V.tensor_copy(out=T.z[:].indirect(T.off1[:, 0:16]), in_=T.qrep[:]))
     wait(P, e_off1)
-    e_l2 = to_list(T.psL[:, 16:32], lambda i: T.w[:, 16 * i:16 * i + 16])
-    wait(S_, e_by)
-    e_bo = [do(S_.activation(T.boff[:, b::4], T.by[:, 32 * b:32 * b + 32], COPY)) for b in range(4)]
+    last = []
+    for h in range(2):
+        for i in range(16):
+            m = P.matmul((T.psL, T.psM)[h][:, 128:136], T.b8[half[h], 16 + h - i:144 + h - i], T.w[half[h], 8 * i:8 * i + 8], i == 0, i == 15)
+        last.append(m)
+    e_l2 = do(*last)
+    wait(g, e_neg)
+    e = do(g.affine_select(T.emb[:], T.neg[:], [[-1, 128]], A.is_equal, 0.0, -1, 1))
+    wait(g, e)
+    e_em = do(g.affine_select(T.em[:], T.emb[:], [[-1, 128]], A.not_equal, 1.0, 0, 1))
 
-    def transfer(buf, src_col, dst_col, peer, n, slot, sem):
-        dst = T.cores[peer]
-        rid, pid, _ = topo.addr(dst)
-        en = topo.engines(core, dst)[n * slot:n * slot + n]
-        return RemoteDMATransfer(dst_ids=[DstId(rid=rid, pnc=pid)], dma_engine_mask=sum(1 << x for x in en), remote_sem=sem,
-                                 src=buf[:, src_col:src_col + CAP], dst=buf[:, dst_col:dst_col + CAP])
+    def transfer(src, dst, peer, slot, sem):
+        c = T.cores[peer]
+        rid, pid, _ = topo.addr(c)
+        en = topo.engines(core, c)[4 * slot:4 * slot + 4]
+        return RemoteDMATransfer(dst_ids=[DstId(rid=rid, pnc=pid)], dma_engine_mask=sum(1 << x for x in en), remote_sem=sem, src=src, dst=dst)
 
+    def blk(buf, k):
+        return buf[:, CAP * k:CAP * k + CAP]
+
+    PLACES = ((1, 2, 3), (4, 5, 6, 7))
     wait(g, e_sc)
-    for ks, sem in (((6, 5, 4), T.sem.arrA), ((3, 2, 1, 0), T.sem.arrB)):
-        g.remote_dma_fused([transfer(T.z, CAP * k, S + CAP * (6 - k), (me + 1 + k) % N, 4, j, sem) for j, k in enumerate(ks)],
+    for ks, sem in zip(PLACES, (T.sem.arrA, T.sem.arrB)):
+        g.remote_dma_fused([transfer(blk(T.z, (me - k) % N), blk(T.xs, k), (me - k) % N, j, sem) for j, k in enumerate(ks)],
                            local_sem=T.sem.sent)
     e_go = ev()
     g.sem_inc(e_go, 1)
     wait(SY, (e_go, 1))
-    SY.dma_start(T.nkw[:, NA:M], T.nk[:, NA:M]).then_inc(T.sem.nkin, 16)
-    e_vec = do(SY.dma_start(T.vw[:], T.vec[:]), 16)
+    nk_b = do(SY.dma_start(T.nkw[:, NA:M], T.nk[:, NA:M]), n=16)
+    e_vec = do(SY.dma_start(T.vw[:], T.vec[:]), n=16)
 
-    wait(V, e_sup)
-    e = do(V.memset(T.sup[:, 0::16], 0.0))
-    wait(V, e)
-    e_dm = do(V.tensor_tensor(out=T.dm[:], in0=T.idn[:], in1=T.sup[:], op=A.subtract))
-    wait(V, e_nk0)
-    e_k0 = do(V.tensor_copy(out=T.key0[:], in_=T.nk0[:, 0:1]))
-    wait(V, e_l2)
-    e_off2 = do(V.tensor_copy(out=T.off2[:], in_=T.psL[:, 16:32]))
-    wait(V, kid_in, *e_bo)
-    e_cz = do(V.tensor_copy(out=T.cz[:], in_=T.kids[:].indirect(T.boff[:, 0:2])))
+    wait(S_, e_sc)
+    e_own = do(S_.activation(blk(T.xs, 0), blk(T.z, me), COPY))
+    e_bs = do(ts(T.bsel[:], T.jd[:, 0:144], C16, A.is_equal), ts(T.idn[:], T.jd[:, 0:128], 0.0, A.is_equal))
+    wait(V, kid_in, e_bo)
+    e_l2n = do(V.tensor_copy(out=T.l2[:], in_=T.kids[:].indirect(T.boff[:, 0:2])))
     e_ct = do(V.tensor_copy(out=T.ct[:, 0:16 * VC], in_=T.kids[:].indirect(T.boff[:, 0:VC])))
-    wait(S_, kid_in, *e_bo)
+    wait(V, e_l2)
+    e_off2 = do(*[V.tensor_copy(out=T.off2[:, h::2], in_=(T.psL, T.psM)[h][:, 128:136]) for h in range(2)])
+    wait(V, nk_a)
+    e_k0 = do(V.tensor_copy(out=T.key0[:], in_=T.nkw[:, 0:1]))
+    wait(S_, kid_in, e_bo)
     e_cs = do(S_.activation(T.ct[:, 16 * VC:M], T.kids[:].indirect(T.boff[:, VC:128]), COPY))
-    wait(P, e_cz, e_dm)
-    e_p0 = do(P.matmul(T.psM[:, 256:257], T.dm[:], T.cz[:, 0:1], True, True))
-    wait(V, e_p0)
-    e_d0 = do(V.tensor_copy(out=T.d0[:], in_=T.psM[:, 256:257]))
+    wait(S_, e_ct, e_cs, e_l2n)
+    e_l3 = do(S_.activation(T.l3[:], T.ct[:].indirect(T.l2[:, 0:2]), COPY))
 
-    X = (T.z[:, OWN:OWN + H], T.z[:, OWN + H:OWN + S])
+    X = (T.xs[:, 0:H], T.xs[:, H:S])
     ps = (T.psA, T.psB)
     po = (T.psP, T.psQ)
     arr = ((T.sem.arrA, 12), (T.sem.arrB, 16))
@@ -204,71 +227,79 @@ def rank_program(g, core, T, topo):
     def col(buf, l, h):
         return buf[:, S * l + H * h:S * l + H * h + H]
 
-    def spread(l, h, e_pr):
-        wait(P, e_pr)
+    def to_list(buf, l, h, e_in, first=True):
+        wait(P, e_in)
         b = S * l + H * h
-        return to_list(ps[h][:, 16 * l:16 * l + 12], lambda i: T.pr[:, b + i:b + H:16])
+        for i in range(16):
+            m = P.matmul(ps[h][:, 16 * l:16 * l + 12], T.bsel[:, 15 - i:143 - i], buf[:, b + i:b + H:16], first and i == 0, i == 15)
+        return do(m)
 
-    def offsets(l, h):
-        o = T.offs[:, 32 * (l - 1) + 16 * h:32 * (l - 1) + 16 * h + 12]
+    def offsets(l, h, less=0.0):
+        o = T.offs[:, 32 * l + 16 * h:32 * l + 16 * h + 12]
         wait(V, lst[h])
-        return o, do(V.tensor_copy(out=o, in_=ps[h][:, 16 * (l - 1):16 * (l - 1) + 12]))
+        return o, do(ts(o, ps[h][:, 16 * l:16 * l + 12], -less, A.add))
 
-    def compare(l, h, o, e_o):
-        wait(S_, e_o)
-        if l == 1 and h == 0:
-            wait(S_, e_ct, e_cs)
-        e_g = do(S_.activation(col(T.cg, l, h), T.ct[:].indirect(o), COPY))
+    def compare(keys, l, h, o, e_o):
         wait(V, e_o)
-        if l == 1 and h == 0:
-            wait(V, nk_in)
-        e_c = do(V.tensor_tensor(out=col(T.cmp, l, h), in0=T.nkw[:].indirect(o), in1=X[h], op=A.is_le))
-        wait(P, e_c)
-        return e_g, do(P.matmul(po[h][:, 0:H], T.em[:], col(T.cmp, l, h), True, True))
-
-    def pick(l, h, e_g, e_one):
-        wait(V, e_g, e_one)
-        return do(V.tensor_tensor(out=col(T.pr, l, h), in0=po[h][:, 0:H], in1=col(T.cg, l, h), op=A.mult))
+        return do(V.tensor_tensor(out=col(T.cmp, l, h), in0=keys.indirect(o), in1=X[h], op=A.is_le))
 
     lst = [None, None]
-    wait(V, e_k0, e_d0)
+    wait(V, e_k0, e_own)
+    wait(P, e_bs, e_em)
     for h in range(2):
         wait(V, arr[h])
-        e_pr = do(V.tensor_scalar(out=col(T.pr, 0, h), in0=X[h], scalar1=T.key0[:], scalar2=T.d0[:], op0=A.is_ge, op1=A.mult))
-        lst[h] = spread(0, h, e_pr)
-    for l in range(1, D):
-        es = [compare(l, h, *offsets(l, h)) for h in range(2)]
-        for h in range(2):
-            lst[h] = spread(l, h, pick(l, h, *es[h]))
-    offs = []
+        lst[h] = to_list(T.cmp, 0, h, do(ts(col(T.cmp, 0, h), X[h], T.key0[:], A.is_ge)))
+    wait(V, nk_b, e_l2n)
+    e_k2 = do(V.tensor_copy(out=T.k2[:], in_=T.nkw[:].indirect(T.l2[:, 0:2])))
+    wait(V, e_k2)
     for h in range(2):
-        o, e_o = offsets(D, h)
-        out = OWN + H * h
+        o, e_o = offsets(0, h, 1.0)
+        wait(S_, e_o)
+        u = T.up[:, 16 * h:16 * h + 12]
+        e_up = do(S_.activation(u, o, COPY, bias=-1.0, scale=16.0))
+        e_c = compare(T.k2[:], 1, h, o, e_o)
+        wait(P, e_up)
+        P.matmul(ps[h][:, 16:28], T.idn[:], u, True, False)
+        lst[h] = to_list(T.cmp, 1, h, e_c, first=False)
         if h == 0:
-            wait(S_, e_o, e_vec)
-            e_y = [do(S_.activation(T.yb[:, out:out + H], T.vw[:].indirect(o), COPY))]
+            wait(S_, e_l3, nk_a, nk_b)
+            e_k3 = do(S_.activation(T.k3[:], T.nkw[:].indirect(T.l3[:, 0:16]), COPY))
+    e_c3 = do(S_.activation(T.c3[:], T.ct[:].indirect(T.l3[:, 0:16]), COPY))
+    wait(V, e_k3)
+    wait(S_, e_c3)
+    for l, keys, child in ((2, T.k3, T.c3), (3, T.nkw, T.ct)):
+        es = []
+        for h in range(2):
+            o, e_o = offsets(l - 1, h)
+            wait(S_, e_o)
+            e_g = do(S_.activation(col(T.cg, l, h), child[:].indirect(o), COPY))
+            wait(P, compare(keys[:], l, h, o, e_o))
+            es.append((e_g, do(P.matmul(po[h][:, 0:H], T.em[:], col(T.cmp, l, h), True, True))))
+        for h in range(2):
+            wait(V, *es[h])
+            e_pr = do(V.tensor_tensor(out=col(T.pr, l, h), in0=po[h][:, 0:H], in1=col(T.cg, l, h), op=A.mult))
+            lst[h] = to_list(T.pr, l, h, e_pr)
+    for h in range(2):
+        o, e_o = offsets(D - 1, h)
+        out = H * h
+        wait(S_, e_o, e_vec)
+        if h == 0:
+            e_y = do(S_.activation(T.yo[:, 0:H], T.vw[:].indirect(o), COPY))
+            wait(S_, e_y)
+            e_mine = do(S_.activation(blk(T.ret, me), blk(T.yo, 0), COPY))
         else:
             b = 32 * (D - 1) + 16 * h
-            wait(S_, e_o, e_vec)
-            e_y = [do(S_.activation(T.yb[:, out + H // 2:out + H], T.vw[:].indirect(T.offs[:, b + 6:b + 12]), COPY))]
             wait(V, e_o, e_vec)
-            e_y.append(do(V.tensor_copy(out=T.yb[:, out:out + H // 2], in_=T.vw[:].indirect(T.offs[:, b:b + 6]))))
-        wait(g, *e_y)
-        sem = (T.sem.retA, T.sem.retB)[h]
-        g.remote_dma_fused([transfer(T.yb, S + CAP * k, CAP * (6 - k), (me + 1 + k) % N, 4, j, sem)
-                            for j, k in enumerate(((0, 1, 2), (3, 4, 5, 6))[h])], local_sem=T.sem.sent)
-        offs += e_y
+            e_y = do(S_.activation(T.yo[:, out + H // 2:out + H], T.vw[:].indirect(T.offs[:, b + 6:b + 12]), COPY),
+                     V.tensor_copy(out=T.yo[:, out:out + H // 2], in_=T.vw[:].indirect(T.offs[:, b:b + 6])))
+        wait(g, e_y)
+        g.remote_dma_fused([transfer(blk(T.yo, k), blk(T.ret, me), (me + k) % N, j, (T.sem.retA, T.sem.retB)[h])
+                            for j, k in enumerate(PLACES[h])], local_sem=T.sem.sent)
 
-    for j, (q, dq) in enumerate(((V, SY), (S_, S_))):
-        wait(q, *offs)
-        wait(q, (T.sem.retA, 12), (T.sem.retB, 16), e_off2)
-        c = slice(128 * j, 128 * j + 128)
-        src = T.yb[:, 0:S].indirect(T.off2[:, 8 * j:8 * j + 8])
-        if j == 0:
-            e = do(V.tensor_copy(out=T.ysb[:, c], in_=src))
-        else:
-            e = do(S_.activation(T.ysb[:, c], src, COPY))
-        wait(dq, e)
-        e = do(dq.dma_start(T.y[:, c], T.ysb[:, c]), 16)
-        wait(dq, e)
+    for q in (V, S_):
+        wait(q, e_mine, e_off2, (T.sem.retA, 12), (T.sem.retB, 16))
+    e = do(V.tensor_copy(out=T.ysb[:, 0:128], in_=T.ret[:].indirect(T.off2[:, 0:8])),
+           S_.activation(T.ysb[:, 128:Q], T.ret[:].indirect(T.off2[:, 8:16]), COPY))
+    wait(SY, e)
+    wait(SY, do(SY.dma_start(T.y[:], T.ysb[:]), n=16))
     g.wait_ge(T.sem.sent, 56)

@@ -6,25 +6,32 @@ S = N * CAP
 H = S // 2
 KW = E - 15
 VC = 48
-NA = 1344
+NA = 960
 
 SCRATCH = {
+    "qh": ("sbuf", [128, 128], "int32"),
     "qi": ("sbuf", [128, Q], "int32"),
     "qf": ("sbuf", [128, Q], "float32"),
     "qrep": ("sbuf", [128, Q], "int32"),
     "spc": ("sbuf", [128, 1], "int32"),
-    "lof": ("sbuf", [128, 1], "float32"),
+    "spf": ("sbuf", [128, 1], "float32"),
     "kp": ("sbuf", [128, 1], "int32"),
-    "kq": ("sbuf", [128, 8], "int32"),
+    "kq": ("sbuf", [128, 12], "int32"),
     "cols": ("sbuf", [128, 16], "float32"),
-    "sel": ("sbuf", [128, 192], "float32"),
+    "sel": ("sbuf", [128, 128], "float32"),
     "rep": ("sbuf", [128, 128], "float32"),
-    "jd": ("sbuf", [128, 160], "bfloat16"),
-    "ones": ("sbuf", [128, 192], "bfloat16"),
+    "jd": ("sbuf", [128, 144], "bfloat16"),
+    "ones": ("sbuf", [128, 128], "bfloat16"),
     "m3": ("sbuf", [128, 3 * 128], "float16"),
-    "b8": ("sbuf", [128, 160], "float16"),
+    "b8": ("sbuf", [128, 144], "float16"),
+    "b8y": ("sbuf", [128, 144], "float16"),
     "bsel": ("sbuf", [128, 144], "float16"),
-    "neg": ("sbuf", [128, 128], "bfloat16"),
+    "bd": ("sbuf", [128, 144], "float16"),
+    "b16": ("sbuf", [128, 144], "float16"),
+    "dmb": ("sbuf", [128, 128], "bfloat16"),
+    "dm": ("sbuf", [128, 128], "float16"),
+    "cz": ("sbuf", [128, 32], "float16"),
+    "neg": ("sbuf", [128, 144], "bfloat16"),
     "emb": ("sbuf", [128, 128], "bfloat16"),
     "em": ("sbuf", [128, 128], "float16"),
     "idn": ("sbuf", [128, 128], "float16"),
@@ -64,7 +71,7 @@ SCRATCH = {
     "psP": ("psum", [128, 512], "float32"),
     "psQ": ("psum", [128, 512], "float32"),
 }
-SEMAPHORES = ["e%d" % i for i in range(136)] + ["splin", "kidin", "btin", "arrA", "arrB", "retA", "retB", "sent"]
+SEMAPHORES = ["e%d" % i for i in range(136)] + ["qin", "kidin", "btin", "arrA", "arrB", "retA", "retB", "sent"]
 
 
 def rank_program(g, core, T, topo):
@@ -95,129 +102,164 @@ def rank_program(g, core, T, topo):
             return V.tensor_scalar(out=out, in0=in0, scalar1=s1, scalar2=None, op0=op0)
         return V.tensor_scalar(out=out, in0=in0, scalar1=s1, scalar2=s2, op0=op0, op1=op1)
 
+    def act(out, in_, scale=1.0, bias=0.0):
+        return S_.activation(out, in_, COPY if isinstance(bias, float) else IDENT, bias=bias, scale=scale)
+
+    spl_in = do(S_.dma_start(T.spc[0:64, 0:1], T.spl[:]), n=16)
+    def kid_load(o):
+        SY.dma_start(T.kids[o::16, :], T.kid[:, o:o + KW]).then_inc(T.sem.kidin, 16)
+
+    for r in range(N):
+        (SY if r % 2 else S_).dma_start(T.qh[r::8, :], T.q[:]).then_inc(T.sem.qin, 16)
+        if r % 4 == 1:
+            kid_load(r // 4)
     q_in = do(SY.dma_start(T.qi[0:8, :], T.q[:]), n=16)
     for h in range(2):
-        S_.dma_start(T.spc[64 * h:64 * h + 64, 0:1], T.spl[:]).then_inc(T.sem.splin, 16)
-    for h in range(2):
         S_.dma_start(T.bt[:, 64 * h:64 * h + 64], T.beg[h::2, :]).then_inc(T.sem.btin, 16)
-    for o in range(16):
-        SY.dma_start(T.kids[o::16, :], T.kid[:, o:o + KW]).then_inc(T.sem.kidin, 16)
+    for o in range(2, 16):
+        kid_load(o)
     nk_a = do(SY.dma_start(T.nkw[:, 0:NA], T.nk[:, 0:NA]), n=16)
-    spl_in, kid_in, bt_in = (T.sem.splin, 32), (T.sem.kidin, 256), (T.sem.btin, 32)
+    qh_in, kid_in, bt_in = (T.sem.qin, 16 * N), (T.sem.kidin, 256), (T.sem.btin, 32)
 
-    half = (slice(0, 64), slice(64, 128))
-    CA, CB, CC, CU, CI, CT, CS, C16, CR = (T.cols[:, j:j + 1] for j in range(9))
+    CA, CB, CC, SG, U1, U2, U3, U4, CI, CT, CY, C16 = (T.cols[:, j:j + 1] for j in range(12))
+    R, HB, O = T.kq[:, 0:1], T.kq[:, 4:5], T.kq[:, 8:9]
     e_one = do(V.memset(T.ones[:], 1.0))
     e_kp = do(g.iota(T.kp[:], [[0, 1]], 0, 1))
+    e_jd = do(g.iota(T.jd[:], [[1, 144]], 0, -1, allow_small_or_imprecise_dtypes=True))
     wait(g, e_one)
-    e_sel = do(g.affine_select(T.sel[0:8, :], T.ones[0:8, :], [[-1, 24], [0, 8]], A.is_equal, 0.0, 8, 1))
-    e_jd = do(g.iota(T.jd[:], [[1, 160]], 0, -1, allow_small_or_imprecise_dtypes=True))
+    e_sel = do(g.affine_select(T.sel[0:64, :], T.ones[0:64, :], [[-8, 8], [0, 2], [-1, 8]], A.is_equal, 0.0, 0, 1))
+    e_rep = do(g.affine_select(T.rep[0:8, :], T.ones[0:8, :], [[-1, 8], [0, 16]], A.is_equal, 0.0, 0, 1))
     e_z0 = do(g.iota(T.z[:], [[0, S]], 0, 0))
-    e_c0 = do(V.memset(T.cols[half[0], 6:7], 1.0), V.memset(T.cols[half[1], 6:7], -1.0))
     e_neg = do(V.memset(T.neg[:], -1.0))
     wait(V, e_kp)
-    e_kq = do(ts(T.kq[:, 0:1], T.kp[:], 7, A.bitwise_and), ts(T.kq[:, 4:5], T.kp[:], 15, A.bitwise_and))
-    wait(V, e_kq, e_neg)
-    R = T.kq[:, 0:1]
-    e_c1 = do(ts(CA, R, 0.0, A.is_gt, 1.0, A.add), ts(CB, R, 0.0, A.is_gt, -1.0, A.mult), ts(CC, R, 7.0, A.is_lt, -1.0, A.mult))
+    e_kq = do(ts(R, T.kp[:], 7, A.bitwise_and), ts(HB, T.kp[:], 8, A.bitwise_and), ts(O, T.kp[:], 15, A.bitwise_and))
+    wait(V, e_neg)
     e_neg = do(V.memset(T.neg[:, 15::16], 0.0))
     wait(S_, e_kq)
-    e_u = do(*[S_.activation(T.cols[half[h], 3:4], T.kq[half[h], 0:1], COPY, bias=(25.0, 24.0)[h], scale=(-24.0, 24.0)[h]) for h in range(2)],
-             *[S_.activation(T.cols[half[h], 8:9], T.kq[half[h], 0:1], COPY, bias=16.0 - 127.0 * h, scale=-2.0) for h in range(2)])
+    e_u = do(act(SG, HB, -0.25, 1.0), act(U1, R, -24.0, 0.5), act(U2, R, 24.5, -196.0), act(U3, HB, -0.875, 16.0))
 
-    wait(V, q_in)
-    wait(S_, q_in)
-    e_qf = do(V.tensor_copy(out=T.qf[0:8, 0:128], in_=T.qi[0:8, 0:128]), S_.activation(T.qf[0:8, 128:Q], T.qi[0:8, 128:Q], COPY))
-    wait(S_, e_sel, e_u)
-    e_rep = do(*[S_.activation(T.rep[0:8, j::2], T.sel[0:8, 64:128], COPY) for j in range(2)])
-    e_ci = do(S_.activation(CT, T.kp[:], IDENT, bias=CR),
-              *[S_.activation(T.cols[half[h], 4:5], T.kq[half[h], 0:1], COPY, bias=(1336.0, -1728.0)[h], scale=T.cols[half[h], 3:4]) for h in range(2)],
-              S_.activation(C16, T.kq[:, 4:5], COPY, bias=15.0, scale=-1.0))
-    wait(P, e_qf, e_sel)
-    P.matmul(T.psP[:, 0:128], T.sel[0:8, 64:192], T.qf[0:8, 0::2], True, False)
-    e_qh = do(P.matmul(T.psP[:, 0:128], T.sel[0:8, 0:128], T.qf[0:8, 1::2], False, True))
-    wait(P, e_rep)
-    P.matmul(T.psQ[:, 0:128], T.rep[0:8, :], T.qf[0:8, 0:128], True, True)
+    wait(V, e_kq)
+    e_c1 = do(ts(CA, R, 0.0, A.is_gt, 1.0, A.add), ts(CB, R, 0.0, A.is_gt, -1.0, A.mult), ts(CC, R, 7.0, A.is_lt, -1.0, A.mult))
     wait(V, spl_in)
-    e_lo = do(V.tensor_copy(out=T.lof[:], in_=T.spc[:]))
+    e = do(V.tensor_copy(out=T.spf[0:64, :], in_=T.spc[0:64, :]))
+    wait(P, e, e_sel)
+    e_lo = do(P.matmul(T.psP[:, 0:1], T.sel[0:64, :], T.spf[0:64, :], True, True))
+    wait(S_, e_u)
+    e_u4 = do(act(U4, R, U1, 1532.0), act(CT, R, -1.0, U3))
+    e_cy = do(act(CY, R, -1.0, 16.0), act(C16, O, -1.0, 15.0))
+    wait(S_, e_u4)
+    e_ci = do(act(CI, U4, SG, U2))
+    wait(S_, q_in)
+    e_qf = do(act(T.qf[0:8, :], T.qi[0:8, :]))
     wait(V, e_jd, e_c1)
     e_m3 = do(*[ts(T.m3[:, 128 * j:128 * j + 128], T.jd[:, 0:128], float(d), A.is_equal, c, A.mult)
                 for j, (d, c) in enumerate(((0, CA), (-1, CB), (1, CC)))])
-    wait(V, e_lo, e_qh)
-    e_ge = do(ts(T.ge[:], T.psP[:, 0:128], T.lof[:], A.is_ge))
+    wait(V, qh_in, e_lo)
+    e_ge = do(ts(T.ge[:], T.qh[:], T.psP[:, 0:1], A.is_ge))
+    wait(V, e_u, e_u4)
+    e_b8 = do(ts(T.b8[:], T.jd[:], CT, A.is_equal, SG, A.mult))
     wait(P, e_m3, e_ge)
     for j in range(3):
         m = P.matmul(T.psM[:, 0:128], T.m3[:, 128 * j:128 * j + 128], T.ge[:], j == 0, j == 2)
     e_mask = do(m)
-    e_qr = do(P.matmul(T.psQ[:, 128:Q], T.rep[0:8, :], T.qf[0:8, 128:Q], True, True))
-    wait(V, e_ge, e_one, e_ci, e_c0)
-    e = do(V.tensor_tensor_scan(T.cum[:], T.ones[:, 0:128], T.ge[:], CI, A.mult, A.add))
-    e_b8 = do(ts(T.b8[:], T.jd[:], CT, A.is_equal, CS, A.mult))
+    wait(P, e_qf, e_rep)
+    e_qr = [do(P.matmul((T.psQ, T.psA)[h][:, 0:128], T.rep[0:8, :], T.qf[0:8, 128 * h:128 * h + 128], True, True)) for h in range(2)]
+    wait(V, e_one, e_ci, e_ge)
+    e = do(V.tensor_tensor_scan(T.cum[:], T.ones[:], T.ge[:], CI, A.mult, A.add))
+    wait(V, e_cy)
+    e_b8y = do(ts(T.b8y[:], T.jd[:], CY, A.is_equal, SG, A.mult))
+    e_bs = do(ts(T.bsel[:], T.jd[:], C16, A.is_equal))
     wait(V, e, e_mask)
     e_w = do(V.tensor_tensor(out=T.w[:], in0=T.psM[:, 0:128], in1=T.cum[:], op=A.mult))
-    wait(P, e_w, e_b8)
+    wait(P, e_b8, e_w)
     for i in range(8):
         m = P.matmul(T.psL[:, 0:16], T.b8[:, 16 - 2 * i:144 - 2 * i], T.w[:, i::8], i == 0, i == 7)
     e_l1 = do(m)
+    wait(P, e_b8y)
+    for i in range(8):
+        m = P.matmul(T.psM[:, 128:144], T.b8y[:, 16 - i:144 - i], T.w[:, 16 * i:16 * i + 16], i == 0, i == 7)
+    e_l2 = do(m)
     wait(S_, bt_in)
-    e_bx = do(*[S_.activation(T.bx[:, 32 * b + 16 * h:32 * b + 16 * h + 16], T.bt[:, 64 * h + 16 * b:64 * h + 16 * b + 16], COPY)
+    e_bx = do(*[act(T.bx[:, 32 * b + 16 * h:32 * b + 16 * h + 16], T.bt[:, 64 * h + 16 * b:64 * h + 16 * b + 16])
                 for h in range(2) for b in range(4)])
+    e_ev = []
+    for h in range(2):
+        wait(S_, e_qr[h])
+        e_ev.append(act(T.qrep[:, h::2], (T.psQ, T.psA)[h][:, 0:128]))
+    e_ev = do(*e_ev)
     wait(V, e_bx)
     e_by = do(V.transpose(T.by[:], T.bx[:]))
-    wait(S_, e_qr)
-    e_ev = do(S_.activation(T.qrep[:], T.psQ[:, 0:Q], COPY))
     wait(S_, e_by)
-    e_bo = do(*[S_.activation(T.boff[:, b::4], T.by[:, 32 * b:32 * b + 32], COPY) for b in range(4)])
+    e_bo = do(*[act(T.boff[:, b::4], T.by[:, 32 * b:32 * b + 32]) for b in range(4)])
+    wait(S_, e_bs)
+    e_bs = do(act(T.b16[:], T.bsel[:], 16.0))
     wait(V, e_l1)
     e_off1 = do(V.tensor_copy(out=T.off1[:], in_=T.psL[:, 0:16]))
-    wait(V, e_off1, e_z0, e_ev)
+    wait(V, e_l2)
+    e_off2 = do(V.tensor_copy(out=T.off2[:], in_=T.psM[:, 128:144]))
+    wait(V, e_z0, e_ev, e_off1)
     e_sc = do(V.tensor_copy(out=T.z[:].indirect(T.off1[:, 0:16]), in_=T.qrep[:]))
-    wait(P, e_off1)
-    last = []
-    for h in range(2):
-        for i in range(16):
-            m = P.matmul((T.psL, T.psM)[h][:, 128:136], T.b8[half[h], 16 + h - i:144 + h - i], T.w[half[h], 8 * i:8 * i + 8], i == 0, i == 15)
-        last.append(m)
-    e_l2 = do(*last)
     wait(g, e_neg)
-    e = do(g.affine_select(T.emb[:], T.neg[:], [[-1, 128]], A.is_equal, 0.0, -1, 1))
+    e_emb = do(g.affine_select(T.emb[:], T.neg[:, 0:128], [[-1, 128]], A.is_equal, 0.0, -1, 1))
+    e = do(g.affine_select(T.dmb[:], T.neg[:, 15:143], [[-1, 128]], A.is_equal, 0.0, 1, 1))
     wait(g, e)
-    e_em = do(g.affine_select(T.em[:], T.emb[:], [[-1, 128]], A.not_equal, 1.0, 0, 1))
+    e_dm = do(g.affine_select(T.dm[:], T.dmb[:], [[-1, 128]], A.not_equal, 1.0, 0, 1))
 
-    def transfer(src, dst, peer, slot, sem):
+    def transfer(src, dst, peer, slot, sem, of=4):
         c = T.cores[peer]
         rid, pid, _ = topo.addr(c)
-        en = topo.engines(core, c)[4 * slot:4 * slot + 4]
+        en = topo.engines(core, c)
+        if of > 1:
+            en = en[slot % 2::2]
+        if of > 2:
+            en = en[4 * (slot // 2):4 * (slot // 2) + 4]
         return RemoteDMATransfer(dst_ids=[DstId(rid=rid, pnc=pid)], dma_engine_mask=sum(1 << x for x in en), remote_sem=sem, src=src, dst=dst)
 
     def blk(buf, k):
         return buf[:, CAP * k:CAP * k + CAP]
 
+    near = [r for r in range(N) if topo.die(T.cores[r]) == topo.die(core)]
+    far = [r for r in range(N) if r not in near]
+    STEP = {1: (1, 0), 2: (0, 1), 3: (1, 1), 4: (1, 2), 5: (0, 2), 6: (1, 3), 7: (0, 3)}
+
+    def peer(k, sign):
+        other, step = STEP[k]
+        side = far if other else near
+        return side[(near.index(me) + sign * step) % len(side)]
+
     PLACES = ((1, 2, 3), (4, 5, 6, 7))
+    RETURNS = (((1, 2, 3),), ((4, 5, 6, 7),))
     wait(g, e_sc)
-    for ks, sem in zip(PLACES, (T.sem.arrA, T.sem.arrB)):
-        g.remote_dma_fused([transfer(blk(T.z, (me - k) % N), blk(T.xs, k), (me - k) % N, j, sem) for j, k in enumerate(ks)],
-                           local_sem=T.sem.sent)
+    for h in range(2):
+        for ks in (PLACES[h],):
+            g.remote_dma_fused([transfer(blk(T.z, peer(k, 1)), blk(T.xs, k), peer(k, 1), j, (T.sem.arrA, T.sem.arrB)[h], len(ks))
+                                for j, k in enumerate(ks)], local_sem=T.sem.sent)
     e_go = ev()
     g.sem_inc(e_go, 1)
+    wait(g, e_emb)
+    e_em = do(g.affine_select(T.em[:], T.emb[:], [[-1, 128]], A.not_equal, 1.0, 0, 1))
     wait(SY, (e_go, 1))
-    nk_b = do(SY.dma_start(T.nkw[:, NA:M], T.nk[:, NA:M]), n=16)
+    nk_in = [nk_a, do(SY.dma_start(T.nkw[:, NA:M], T.nk[:, NA:M]), n=16)]
     e_vec = do(SY.dma_start(T.vw[:], T.vec[:]), n=16)
 
-    wait(S_, e_sc)
-    e_own = do(S_.activation(blk(T.xs, 0), blk(T.z, me), COPY))
-    e_bs = do(ts(T.bsel[:], T.jd[:, 0:144], C16, A.is_equal), ts(T.idn[:], T.jd[:, 0:128], 0.0, A.is_equal))
     wait(V, kid_in, e_bo)
+    e_cz = do(V.tensor_copy(out=T.cz[:], in_=T.kids[:].indirect(T.boff[:, 0:2])))
     e_l2n = do(V.tensor_copy(out=T.l2[:], in_=T.kids[:].indirect(T.boff[:, 0:2])))
     e_ct = do(V.tensor_copy(out=T.ct[:, 0:16 * VC], in_=T.kids[:].indirect(T.boff[:, 0:VC])))
-    wait(V, e_l2)
-    e_off2 = do(*[V.tensor_copy(out=T.off2[:, h::2], in_=(T.psL, T.psM)[h][:, 128:136]) for h in range(2)])
+    wait(P, e_cz, e_dm)
+    e_d0 = do(P.matmul(T.psP[:, 0:1], T.dm[:], T.cz[:, 0:1], True, True))
+    wait(V, e_d0)
+    e_bd = do(ts(T.bd[:], T.jd[:], C16, A.is_equal, T.psP[:, 0:1], A.mult))
+    wait(V, e_sc)
+    e_own = do(V.tensor_copy(out=blk(T.xs, 0), in_=blk(T.z, me)))
     wait(V, nk_a)
     e_k0 = do(V.tensor_copy(out=T.key0[:], in_=T.nkw[:, 0:1]))
     wait(S_, kid_in, e_bo)
-    e_cs = do(S_.activation(T.ct[:, 16 * VC:M], T.kids[:].indirect(T.boff[:, VC:128]), COPY))
+    e_cs = do(act(T.ct[:, 16 * VC:M], T.kids[:].indirect(T.boff[:, VC:128])))
     wait(S_, e_ct, e_cs, e_l2n)
-    e_l3 = do(S_.activation(T.l3[:], T.ct[:].indirect(T.l2[:, 0:2]), COPY))
+    e_l3 = do(act(T.l3[:], T.ct[:].indirect(T.l2[:, 0:2])))
+    wait(S_, e_l3)
+    e_c3 = do(act(T.c3[:], T.ct[:].indirect(T.l3[:, 0:16])))
 
     X = (T.xs[:, 0:H], T.xs[:, H:S])
     ps = (T.psA, T.psB)
@@ -227,17 +269,27 @@ def rank_program(g, core, T, topo):
     def col(buf, l, h):
         return buf[:, S * l + H * h:S * l + H * h + H]
 
-    def to_list(buf, l, h, e_in, first=True):
-        wait(P, e_in)
-        b = S * l + H * h
-        for i in range(16):
-            m = P.matmul(ps[h][:, 16 * l:16 * l + 12], T.bsel[:, 15 - i:143 - i], buf[:, b + i:b + H:16], first and i == 0, i == 15)
-        return do(m)
+    def sums(l, h):
+        return ((T.psL, T.psM) if l == 1 else ps)[h][:, 256 + 16 * l:256 + 16 * l + 12]
 
-    def offsets(l, h, less=0.0):
+    def to_list(buf, lb, l, h, e_in, first=True, last=True, sel=T.bsel):
+        b = S * lb + H * h
+        for u in range(2):
+            wait(P, e_in[u])
+            for i in range(u, 16, 2):
+                m = P.matmul(sums(l, h), sel[:, 15 - i:143 - i], buf[:, b + i:b + H:16], first and i == 0, last and i == 15)
+        return do(m) if last else None
+
+    def odd(buf, l, h, u):
+        return buf[:, S * l + H * h + u:S * l + H * h + H:2]
+
+    def offsets(l, h, q=V):
         o = T.offs[:, 32 * l + 16 * h:32 * l + 16 * h + 12]
-        wait(V, lst[h])
-        return o, do(ts(o, ps[h][:, 16 * l:16 * l + 12], -less, A.add))
+        less = 17.0 if l == 1 else 0.0
+        wait(q, lst[h])
+        if q is V:
+            return o, do(ts(o, sums(l, h), -less, A.add))
+        return o, do(S_.activation(o, sums(l, h), ActivationFunctionType.Relu, bias=-less))
 
     def compare(keys, l, h, o, e_o):
         wait(V, e_o)
@@ -245,61 +297,57 @@ def rank_program(g, core, T, topo):
 
     lst = [None, None]
     wait(V, e_k0, e_own)
-    wait(P, e_bs, e_em)
+    wait(P, e_bs, e_off2, e_bd)
     for h in range(2):
         wait(V, arr[h])
-        lst[h] = to_list(T.cmp, 0, h, do(ts(col(T.cmp, 0, h), X[h], T.key0[:], A.is_ge)))
-    wait(V, nk_b, e_l2n)
-    e_k2 = do(V.tensor_copy(out=T.k2[:], in_=T.nkw[:].indirect(T.l2[:, 0:2])))
-    wait(V, e_k2)
+        e_c = [do(ts(col(T.cmp, 0, h), X[h], T.key0[:], A.is_ge))] * 2
+        lst[h] = to_list(T.cmp, 0, 0, h, e_c, sel=T.bd)
+        to_list(T.cmp, 0, 1, h, e_c, last=False, sel=T.b16)
     for h in range(2):
-        o, e_o = offsets(0, h, 1.0)
-        wait(S_, e_o)
-        u = T.up[:, 16 * h:16 * h + 12]
-        e_up = do(S_.activation(u, o, COPY, bias=-1.0, scale=16.0))
-        e_c = compare(T.k2[:], 1, h, o, e_o)
-        wait(P, e_up)
-        P.matmul(ps[h][:, 16:28], T.idn[:], u, True, False)
-        lst[h] = to_list(T.cmp, 1, h, e_c, first=False)
-        if h == 0:
-            wait(S_, e_l3, nk_a, nk_b)
-            e_k3 = do(S_.activation(T.k3[:], T.nkw[:].indirect(T.l3[:, 0:16]), COPY))
-    e_c3 = do(S_.activation(T.c3[:], T.ct[:].indirect(T.l3[:, 0:16]), COPY))
-    wait(V, e_k3)
+        o, e_o = offsets(0, h, (V, S_)[h])
+        wait(V, *nk_in)
+        lst[h] = to_list(T.cmp, 1, 1, h, [compare(T.nkw[:], 1, h, o, e_o)] * 2, first=False)
+    wait(S_, *nk_in)
+    e_k3 = do(act(T.k3[:], T.nkw[:].indirect(T.l3[:, 0:16])))
     wait(S_, e_c3)
+    wait(P, e_em)
     for l, keys, child in ((2, T.k3, T.c3), (3, T.nkw, T.ct)):
         es = []
+        both = [offsets(l - 1, h, (V, S_)[h]) for h in range(2)]
         for h in range(2):
-            o, e_o = offsets(l - 1, h)
+            o, e_o = both[h]
+            wait(V, e_k3)
             wait(S_, e_o)
-            e_g = do(S_.activation(col(T.cg, l, h), child[:].indirect(o), COPY))
+            e_g = do(act(col(T.cg, l, h), child[:].indirect(o)))
             wait(P, compare(keys[:], l, h, o, e_o))
             es.append((e_g, do(P.matmul(po[h][:, 0:H], T.em[:], col(T.cmp, l, h), True, True))))
         for h in range(2):
             wait(V, *es[h])
-            e_pr = do(V.tensor_tensor(out=col(T.pr, l, h), in0=po[h][:, 0:H], in1=col(T.cg, l, h), op=A.mult))
-            lst[h] = to_list(T.pr, l, h, e_pr)
+            e_pr = [do(V.tensor_tensor(out=odd(T.pr, l, h, u), in0=po[h][:, u:H:2], in1=odd(T.cg, l, h, u), op=A.mult)) for u in range(2)]
+            lst[h] = to_list(T.pr, l, l, h, e_pr)
+    wait(S_, e_vec)
     for h in range(2):
         o, e_o = offsets(D - 1, h)
         out = H * h
-        wait(S_, e_o, e_vec)
+        wait(S_, e_o)
+        b = 32 * (D - 1) + 16 * h
         if h == 0:
-            e_y = do(S_.activation(T.yo[:, 0:H], T.vw[:].indirect(o), COPY))
-            wait(S_, e_y)
-            e_mine = do(S_.activation(blk(T.ret, me), blk(T.yo, 0), COPY))
+            e_y = e_ya = do(act(T.yo[:, 0:H], T.vw[:].indirect(o)))
         else:
-            b = 32 * (D - 1) + 16 * h
-            wait(V, e_o, e_vec)
-            e_y = do(S_.activation(T.yo[:, out + H // 2:out + H], T.vw[:].indirect(T.offs[:, b + 6:b + 12]), COPY),
+            wait(V, e_vec, e_o)
+            e_y = do(act(T.yo[:, out + H // 2:out + H], T.vw[:].indirect(T.offs[:, b + 6:b + 12])),
                      V.tensor_copy(out=T.yo[:, out:out + H // 2], in_=T.vw[:].indirect(T.offs[:, b:b + 6])))
         wait(g, e_y)
-        g.remote_dma_fused([transfer(blk(T.yo, k), blk(T.ret, me), (me + k) % N, j, (T.sem.retA, T.sem.retB)[h])
-                            for j, k in enumerate(PLACES[h])], local_sem=T.sem.sent)
+        for ks in RETURNS[h]:
+            g.remote_dma_fused([transfer(blk(T.yo, k), blk(T.ret, me), peer(k, -1), j, (T.sem.retA, T.sem.retB)[h], len(ks))
+                                for j, k in enumerate(ks)], local_sem=T.sem.sent)
 
+    wait(S_, e_ya)
+    e_mine = do(act(blk(T.ret, me), blk(T.yo, 0)))
     for q in (V, S_):
         wait(q, e_mine, e_off2, (T.sem.retA, 12), (T.sem.retB, 16))
     e = do(V.tensor_copy(out=T.ysb[:, 0:128], in_=T.ret[:].indirect(T.off2[:, 0:8])),
-           S_.activation(T.ysb[:, 128:Q], T.ret[:].indirect(T.off2[:, 8:16]), COPY))
+           act(T.ysb[:, 128:Q], T.ret[:].indirect(T.off2[:, 8:16])))
     wait(SY, e)
     wait(SY, do(SY.dma_start(T.y[:], T.ysb[:]), n=16))
     g.wait_ge(T.sem.sent, 56)

from concourse.bass import DstId, RemoteDMATransfer
from concourse.mybir import dt, AluOpType, ActivationFunctionType

N, Q, CAP, M, E, D = 8, 256, 48, 2048, 4096, 4
S = N * CAP
H = S // 2
KW = E - 15
VC = 48
NA = 960

SCRATCH = {
    "qh": ("sbuf", [128, 128], "int32"),
    "qi": ("sbuf", [128, Q], "int32"),
    "qf": ("sbuf", [128, Q], "float32"),
    "qrep": ("sbuf", [128, Q], "int32"),
    "spc": ("sbuf", [128, 1], "int32"),
    "spf": ("sbuf", [128, 1], "float32"),
    "kp": ("sbuf", [128, 1], "int32"),
    "kq": ("sbuf", [128, 12], "int32"),
    "cols": ("sbuf", [128, 16], "float32"),
    "sel": ("sbuf", [128, 128], "float32"),
    "rep": ("sbuf", [128, 128], "float32"),
    "jd": ("sbuf", [128, 144], "bfloat16"),
    "ones": ("sbuf", [128, 128], "bfloat16"),
    "m3": ("sbuf", [128, 3 * 128], "float16"),
    "b8": ("sbuf", [128, 144], "float16"),
    "b8y": ("sbuf", [128, 144], "float16"),
    "bsel": ("sbuf", [128, 144], "float16"),
    "bd": ("sbuf", [128, 144], "float16"),
    "b16": ("sbuf", [128, 144], "float16"),
    "dmb": ("sbuf", [128, 128], "bfloat16"),
    "dm": ("sbuf", [128, 128], "float16"),
    "cz": ("sbuf", [128, 32], "float16"),
    "neg": ("sbuf", [128, 144], "bfloat16"),
    "emb": ("sbuf", [128, 128], "bfloat16"),
    "em": ("sbuf", [128, 128], "float16"),
    "idn": ("sbuf", [128, 128], "float16"),
    "ge": ("sbuf", [128, 128], "float16"),
    "cum": ("sbuf", [128, 128], "float16"),
    "w": ("sbuf", [128, 128], "float16"),
    "off1": ("sbuf", [128, 16], "uint16"),
    "off2": ("sbuf", [128, 16], "uint16"),
    "z": ("sbuf", [128, S], "int32"),
    "xs": ("sbuf", [128, S], "int32"),
    "kids": ("sbuf", [128, KW], "int32"),
    "bt": ("sbuf", [128, 128], "int32"),
    "bx": ("sbuf", [128, 128], "float32"),
    "by": ("sbuf", [128, 128], "float32"),
    "boff": ("sbuf", [128, 128], "uint16"),
    "l2": ("sbuf", [128, 32], "uint16"),
    "l3": ("sbuf", [128, 32], "uint16"),
    "k2": ("sbuf", [128, 32], "int32"),
    "k3": ("sbuf", [128, 256], "int32"),
    "c3": ("sbuf", [128, 256], "float32"),
    "ct": ("sbuf", [128, M], "float32"),
    "key0": ("sbuf", [128, 1], "float32"),
    "nkw": ("sbuf", [128, M], "int32"),
    "vw": ("sbuf", [128, M], "bfloat16"),
    "cmp": ("sbuf", [128, D * S], "float16"),
    "cg": ("sbuf", [128, D * S], "float16"),
    "pr": ("sbuf", [128, D * S], "float16"),
    "up": ("sbuf", [128, 32], "float16"),
    "offs": ("sbuf", [128, D * 32], "uint16"),
    "yo": ("sbuf", [128, S], "bfloat16"),
    "ret": ("sbuf", [128, S], "bfloat16"),
    "ysb": ("sbuf", [128, Q], "bfloat16"),
    "psM": ("psum", [128, 512], "float32"),
    "psL": ("psum", [128, 512], "float32"),
    "psA": ("psum", [128, 512], "float32"),
    "psB": ("psum", [128, 512], "float32"),
    "psP": ("psum", [128, 512], "float32"),
    "psQ": ("psum", [128, 512], "float32"),
}
SEMAPHORES = ["e%d" % i for i in range(136)] + ["qin", "kidin", "btin", "arrA", "arrB", "retA", "retB", "sent"]


def rank_program(g, core, T, topo):
    me = T.rank_of(core)
    if me is None:
        return
    A = AluOpType
    V, P, S_, SY = g.vector, g.tensor, g.scalar, g.sync
    COPY, IDENT = ActivationFunctionType.Copy, ActivationFunctionType.Identity
    cnt = [0]

    def ev():
        cnt[0] += 1
        return T.sem["e%d" % (cnt[0] - 1)]

    def do(*instrs, n=1):
        e = ev()
        for i in instrs:
            i.then_inc(e, n)
        return (e, n * len(instrs))

    def wait(q, *events):
        for e, n in events:
            q.wait_ge(e, n)

    def ts(out, in0, s1, op0, s2=None, op1=None):
        if op1 is None:
            return V.tensor_scalar(out=out, in0=in0, scalar1=s1, scalar2=None, op0=op0)
        return V.tensor_scalar(out=out, in0=in0, scalar1=s1, scalar2=s2, op0=op0, op1=op1)

    def act(out, in_, scale=1.0, bias=0.0):
        return S_.activation(out, in_, COPY if isinstance(bias, float) else IDENT, bias=bias, scale=scale)

    spl_in = do(S_.dma_start(T.spc[0:64, 0:1], T.spl[:]), n=16)
    def kid_load(o):
        SY.dma_start(T.kids[o::16, :], T.kid[:, o:o + KW]).then_inc(T.sem.kidin, 16)

    for r in range(N):
        (SY if r % 2 else S_).dma_start(T.qh[r::8, :], T.q[:]).then_inc(T.sem.qin, 16)
        if r % 4 == 1:
            kid_load(r // 4)
    q_in = do(SY.dma_start(T.qi[0:8, :], T.q[:]), n=16)
    for h in range(2):
        S_.dma_start(T.bt[:, 64 * h:64 * h + 64], T.beg[h::2, :]).then_inc(T.sem.btin, 16)
    for o in range(2, 16):
        kid_load(o)
    nk_a = do(SY.dma_start(T.nkw[:, 0:NA], T.nk[:, 0:NA]), n=16)
    qh_in, kid_in, bt_in = (T.sem.qin, 16 * N), (T.sem.kidin, 256), (T.sem.btin, 32)

    CA, CB, CC, SG, U1, U2, U3, U4, CI, CT, CY, C16 = (T.cols[:, j:j + 1] for j in range(12))
    R, HB, O = T.kq[:, 0:1], T.kq[:, 4:5], T.kq[:, 8:9]
    e_one = do(V.memset(T.ones[:], 1.0))
    e_kp = do(g.iota(T.kp[:], [[0, 1]], 0, 1))
    e_jd = do(g.iota(T.jd[:], [[1, 144]], 0, -1, allow_small_or_imprecise_dtypes=True))
    wait(g, e_one)
    e_sel = do(g.affine_select(T.sel[0:64, :], T.ones[0:64, :], [[-8, 8], [0, 2], [-1, 8]], A.is_equal, 0.0, 0, 1))
    e_rep = do(g.affine_select(T.rep[0:8, :], T.ones[0:8, :], [[-1, 8], [0, 16]], A.is_equal, 0.0, 0, 1))
    e_z0 = do(g.iota(T.z[:], [[0, S]], 0, 0))
    e_neg = do(V.memset(T.neg[:], -1.0))
    wait(V, e_kp)
    e_kq = do(ts(R, T.kp[:], 7, A.bitwise_and), ts(HB, T.kp[:], 8, A.bitwise_and), ts(O, T.kp[:], 15, A.bitwise_and))
    wait(V, e_neg)
    e_neg = do(V.memset(T.neg[:, 15::16], 0.0))
    wait(S_, e_kq)
    e_u = do(act(SG, HB, -0.25, 1.0), act(U1, R, -24.0, 0.5), act(U2, R, 24.5, -196.0), act(U3, HB, -0.875, 16.0))

    wait(V, e_kq)
    e_c1 = do(ts(CA, R, 0.0, A.is_gt, 1.0, A.add), ts(CB, R, 0.0, A.is_gt, -1.0, A.mult), ts(CC, R, 7.0, A.is_lt, -1.0, A.mult))
    wait(V, spl_in)
    e = do(V.tensor_copy(out=T.spf[0:64, :], in_=T.spc[0:64, :]))
    wait(P, e, e_sel)
    e_lo = do(P.matmul(T.psP[:, 0:1], T.sel[0:64, :], T.spf[0:64, :], True, True))
    wait(S_, e_u)
    e_u4 = do(act(U4, R, U1, 1532.0), act(CT, R, -1.0, U3))
    e_cy = do(act(CY, R, -1.0, 16.0), act(C16, O, -1.0, 15.0))
    wait(S_, e_u4)
    e_ci = do(act(CI, U4, SG, U2))
    wait(S_, q_in)
    e_qf = do(act(T.qf[0:8, :], T.qi[0:8, :]))
    wait(V, e_jd, e_c1)
    e_m3 = do(*[ts(T.m3[:, 128 * j:128 * j + 128], T.jd[:, 0:128], float(d), A.is_equal, c, A.mult)
                for j, (d, c) in enumerate(((0, CA), (-1, CB), (1, CC)))])
    wait(V, qh_in, e_lo)
    e_ge = do(ts(T.ge[:], T.qh[:], T.psP[:, 0:1], A.is_ge))
    wait(V, e_u, e_u4)
    e_b8 = do(ts(T.b8[:], T.jd[:], CT, A.is_equal, SG, A.mult))
    wait(P, e_m3, e_ge)
    for j in range(3):
        m = P.matmul(T.psM[:, 0:128], T.m3[:, 128 * j:128 * j + 128], T.ge[:], j == 0, j == 2)
    e_mask = do(m)
    wait(P, e_qf, e_rep)
    e_qr = [do(P.matmul((T.psQ, T.psA)[h][:, 0:128], T.rep[0:8, :], T.qf[0:8, 128 * h:128 * h + 128], True, True)) for h in range(2)]
    wait(V, e_one, e_ci, e_ge)
    e = do(V.tensor_tensor_scan(T.cum[:], T.ones[:], T.ge[:], CI, A.mult, A.add))
    wait(V, e_cy)
    e_b8y = do(ts(T.b8y[:], T.jd[:], CY, A.is_equal, SG, A.mult))
    e_bs = do(ts(T.bsel[:], T.jd[:], C16, A.is_equal))
    wait(V, e, e_mask)
    e_w = do(V.tensor_tensor(out=T.w[:], in0=T.psM[:, 0:128], in1=T.cum[:], op=A.mult))
    wait(P, e_b8, e_w)
    for i in range(8):
        m = P.matmul(T.psL[:, 0:16], T.b8[:, 16 - 2 * i:144 - 2 * i], T.w[:, i::8], i == 0, i == 7)
    e_l1 = do(m)
    wait(P, e_b8y)
    for i in range(8):
        m = P.matmul(T.psM[:, 128:144], T.b8y[:, 16 - i:144 - i], T.w[:, 16 * i:16 * i + 16], i == 0, i == 7)
    e_l2 = do(m)
    wait(S_, bt_in)
    e_bx = do(*[act(T.bx[:, 32 * b + 16 * h:32 * b + 16 * h + 16], T.bt[:, 64 * h + 16 * b:64 * h + 16 * b + 16])
                for h in range(2) for b in range(4)])
    e_ev = []
    for h in range(2):
        wait(S_, e_qr[h])
        e_ev.append(act(T.qrep[:, h::2], (T.psQ, T.psA)[h][:, 0:128]))
    e_ev = do(*e_ev)
    wait(V, e_bx)
    e_by = do(V.transpose(T.by[:], T.bx[:]))
    wait(S_, e_by)
    e_bo = do(*[act(T.boff[:, b::4], T.by[:, 32 * b:32 * b + 32]) for b in range(4)])
    wait(S_, e_bs)
    e_bs = do(act(T.b16[:], T.bsel[:], 16.0))
    wait(V, e_l1)
    e_off1 = do(V.tensor_copy(out=T.off1[:], in_=T.psL[:, 0:16]))
    wait(V, e_l2)
    e_off2 = do(V.tensor_copy(out=T.off2[:], in_=T.psM[:, 128:144]))
    wait(V, e_z0, e_ev, e_off1)
    e_sc = do(V.tensor_copy(out=T.z[:].indirect(T.off1[:, 0:16]), in_=T.qrep[:]))
    wait(g, e_neg)
    e_emb = do(g.affine_select(T.emb[:], T.neg[:, 0:128], [[-1, 128]], A.is_equal, 0.0, -1, 1))
    e = do(g.affine_select(T.dmb[:], T.neg[:, 15:143], [[-1, 128]], A.is_equal, 0.0, 1, 1))
    wait(g, e)
    e_dm = do(g.affine_select(T.dm[:], T.dmb[:], [[-1, 128]], A.not_equal, 1.0, 0, 1))

    def transfer(src, dst, peer, slot, sem, of=4):
        c = T.cores[peer]
        rid, pid, _ = topo.addr(c)
        en = topo.engines(core, c)
        if of > 1:
            en = en[slot % 2::2]
        if of > 2:
            en = en[4 * (slot // 2):4 * (slot // 2) + 4]
        return RemoteDMATransfer(dst_ids=[DstId(rid=rid, pnc=pid)], dma_engine_mask=sum(1 << x for x in en), remote_sem=sem, src=src, dst=dst)

    def blk(buf, k):
        return buf[:, CAP * k:CAP * k + CAP]

    near = [r for r in range(N) if topo.die(T.cores[r]) == topo.die(core)]
    far = [r for r in range(N) if r not in near]
    STEP = {1: (1, 0), 2: (0, 1), 3: (1, 1), 4: (1, 2), 5: (0, 2), 6: (1, 3), 7: (0, 3)}

    def peer(k, sign):
        other, step = STEP[k]
        side = far if other else near
        return side[(near.index(me) + sign * step) % len(side)]

    PLACES = ((1, 2, 3), (4, 5, 6, 7))
    RETURNS = (((1, 2, 3),), ((4, 5, 6, 7),))
    wait(g, e_sc)
    for h in range(2):
        for ks in (PLACES[h],):
            g.remote_dma_fused([transfer(blk(T.z, peer(k, 1)), blk(T.xs, k), peer(k, 1), j, (T.sem.arrA, T.sem.arrB)[h], len(ks))
                                for j, k in enumerate(ks)], local_sem=T.sem.sent)
    e_go = ev()
    g.sem_inc(e_go, 1)
    wait(g, e_emb)
    e_em = do(g.affine_select(T.em[:], T.emb[:], [[-1, 128]], A.not_equal, 1.0, 0, 1))
    wait(SY, (e_go, 1))
    nk_in = [nk_a, do(SY.dma_start(T.nkw[:, NA:M], T.nk[:, NA:M]), n=16)]
    e_vec = do(SY.dma_start(T.vw[:], T.vec[:]), n=16)

    wait(V, kid_in, e_bo)
    e_cz = do(V.tensor_copy(out=T.cz[:], in_=T.kids[:].indirect(T.boff[:, 0:2])))
    e_l2n = do(V.tensor_copy(out=T.l2[:], in_=T.kids[:].indirect(T.boff[:, 0:2])))
    e_ct = do(V.tensor_copy(out=T.ct[:, 0:16 * VC], in_=T.kids[:].indirect(T.boff[:, 0:VC])))
    wait(P, e_cz, e_dm)
    e_d0 = do(P.matmul(T.psP[:, 0:1], T.dm[:], T.cz[:, 0:1], True, True))
    wait(V, e_d0)
    e_bd = do(ts(T.bd[:], T.jd[:], C16, A.is_equal, T.psP[:, 0:1], A.mult))
    wait(V, e_sc)
    e_own = do(V.tensor_copy(out=blk(T.xs, 0), in_=blk(T.z, me)))
    wait(V, nk_a)
    e_k0 = do(V.tensor_copy(out=T.key0[:], in_=T.nkw[:, 0:1]))
    wait(S_, kid_in, e_bo)
    e_cs = do(act(T.ct[:, 16 * VC:M], T.kids[:].indirect(T.boff[:, VC:128])))
    wait(S_, e_ct, e_cs, e_l2n)
    e_l3 = do(act(T.l3[:], T.ct[:].indirect(T.l2[:, 0:2])))
    wait(S_, e_l3)
    e_c3 = do(act(T.c3[:], T.ct[:].indirect(T.l3[:, 0:16])))

    X = (T.xs[:, 0:H], T.xs[:, H:S])
    ps = (T.psA, T.psB)
    po = (T.psP, T.psQ)
    arr = ((T.sem.arrA, 12), (T.sem.arrB, 16))

    def col(buf, l, h):
        return buf[:, S * l + H * h:S * l + H * h + H]

    def sums(l, h):
        return ((T.psL, T.psM) if l == 1 else ps)[h][:, 256 + 16 * l:256 + 16 * l + 12]

    def to_list(buf, lb, l, h, e_in, first=True, last=True, sel=T.bsel):
        b = S * lb + H * h
        for u in range(2):
            wait(P, e_in[u])
            for i in range(u, 16, 2):
                m = P.matmul(sums(l, h), sel[:, 15 - i:143 - i], buf[:, b + i:b + H:16], first and i == 0, last and i == 15)
        return do(m) if last else None

    def odd(buf, l, h, u):
        return buf[:, S * l + H * h + u:S * l + H * h + H:2]

    def offsets(l, h, q=V):
        o = T.offs[:, 32 * l + 16 * h:32 * l + 16 * h + 12]
        less = 17.0 if l == 1 else 0.0
        wait(q, lst[h])
        if q is V:
            return o, do(ts(o, sums(l, h), -less, A.add))
        return o, do(S_.activation(o, sums(l, h), ActivationFunctionType.Relu, bias=-less))

    def compare(keys, l, h, o, e_o):
        wait(V, e_o)
        return do(V.tensor_tensor(out=col(T.cmp, l, h), in0=keys.indirect(o), in1=X[h], op=A.is_le))

    lst = [None, None]
    wait(V, e_k0, e_own)
    wait(P, e_bs, e_off2, e_bd)
    for h in range(2):
        wait(V, arr[h])
        e_c = [do(ts(col(T.cmp, 0, h), X[h], T.key0[:], A.is_ge))] * 2
        lst[h] = to_list(T.cmp, 0, 0, h, e_c, sel=T.bd)
        to_list(T.cmp, 0, 1, h, e_c, last=False, sel=T.b16)
    for h in range(2):
        o, e_o = offsets(0, h, (V, S_)[h])
        wait(V, *nk_in)
        lst[h] = to_list(T.cmp, 1, 1, h, [compare(T.nkw[:], 1, h, o, e_o)] * 2, first=False)
    wait(S_, *nk_in)
    e_k3 = do(act(T.k3[:], T.nkw[:].indirect(T.l3[:, 0:16])))
    wait(S_, e_c3)
    wait(P, e_em)
    for l, keys, child in ((2, T.k3, T.c3), (3, T.nkw, T.ct)):
        es = []
        both = [offsets(l - 1, h, (V, S_)[h]) for h in range(2)]
        for h in range(2):
            o, e_o = both[h]
            wait(V, e_k3)
            wait(S_, e_o)
            e_g = do(act(col(T.cg, l, h), child[:].indirect(o)))
            wait(P, compare(keys[:], l, h, o, e_o))
            es.append((e_g, do(P.matmul(po[h][:, 0:H], T.em[:], col(T.cmp, l, h), True, True))))
        for h in range(2):
            wait(V, *es[h])
            e_pr = [do(V.tensor_tensor(out=odd(T.pr, l, h, u), in0=po[h][:, u:H:2], in1=odd(T.cg, l, h, u), op=A.mult)) for u in range(2)]
            lst[h] = to_list(T.pr, l, l, h, e_pr)
    wait(S_, e_vec)
    for h in range(2):
        o, e_o = offsets(D - 1, h)
        out = H * h
        wait(S_, e_o)
        b = 32 * (D - 1) + 16 * h
        if h == 0:
            e_y = e_ya = do(act(T.yo[:, 0:H], T.vw[:].indirect(o)))
        else:
            wait(V, e_vec, e_o)
            e_y = do(act(T.yo[:, out + H // 2:out + H], T.vw[:].indirect(T.offs[:, b + 6:b + 12])),
                     V.tensor_copy(out=T.yo[:, out:out + H // 2], in_=T.vw[:].indirect(T.offs[:, b:b + 6])))
        wait(g, e_y)
        for ks in RETURNS[h]:
            g.remote_dma_fused([transfer(blk(T.yo, k), blk(T.ret, me), peer(k, -1), j, (T.sem.retA, T.sem.retB)[h], len(ks))
                                for j, k in enumerate(ks)], local_sem=T.sem.sent)

    wait(S_, e_ya)
    e_mine = do(act(blk(T.ret, me), blk(T.yo, 0)))
    for q in (V, S_):
        wait(q, e_mine, e_off2, (T.sem.retA, 12), (T.sem.retB, 16))
    e = do(V.tensor_copy(out=T.ysb[:, 0:128], in_=T.ret[:].indirect(T.off2[:, 0:8])),
           act(T.ysb[:, 128:Q], T.ret[:].indirect(T.off2[:, 8:16])))
    wait(SY, e)
    wait(SY, do(SY.dma_start(T.y[:], T.ysb[:]), n=16))
    g.wait_ge(T.sem.sent, 56)
